import numpy as np
import ml_dtypes


def mxq(x, axis, fmt="e4m3"):
    dtype, down = {"e4m3": (ml_dtypes.float8_e4m3fn, 7), "e5m2": (ml_dtypes.float8_e5m2, 14)}[fmt]
    v = np.moveaxis(np.asarray(x, np.float32).astype(ml_dtypes.bfloat16).astype(np.float64), axis, -1)
    blocks = v.reshape(v.shape[:-1] + (-1, 32))
    amax = np.abs(blocks).max(-1, keepdims=True)
    byte = np.maximum(np.where(amax > 0, np.frexp(amax)[1] - 1 + 127, 0) - down, 1)
    scale = np.exp2(byte - 127.0)
    codes = (blocks / scale).astype(np.float32).astype(dtype).astype(np.float64)
    return np.moveaxis((codes * scale).reshape(v.shape), -1, axis)


WIDE = False


def mx_kscale(k):
    if not WIDE:
        return np.ones(k)
    levels = np.array([10, -10, 5, -5, 0])
    if k % 512:
        return np.exp2(np.random.permutation(np.resize(levels, k // 32))).repeat(32)
    a = np.empty((k // 512, 16))
    for p in range(k // 512):
        a[p, :8] = np.random.permutation(np.resize(levels, 8))
        for g in range(8):
            far = levels[np.abs(levels - a[p, g]) >= 10]
            a[p, g + 8] = far[np.random.randint(len(far))]
    return np.exp2(a.ravel()).repeat(32)


BF16 = ml_dtypes.bfloat16


def bf(x):
    return np.asarray(x, np.float32).astype(BF16)


def f64(x):
    return np.asarray(x).astype(np.float64)


E2M1 = np.array([0.0, 0.5, 1.0, 1.5, 2.0, 3.0, 4.0, 6.0, -0.0, -0.5, -1.0, -1.5, -2.0, -3.0, -4.0, -6.0])


def pack_weight(w, fmt):
    k, n = w.shape
    w = f64(bf(w)).reshape(k // 32, 32, n)
    amax = np.abs(w).max(1)
    if fmt == "e4m3":
        byte = np.frexp(amax)[1] - 1 + 127 - 7
    else:
        mant, ex = np.frexp(amax / 6.0)
        byte = np.where(mant > 0.5, ex, ex - 1) + 127
    byte = np.clip(np.where(amax > 0, byte, 1), 1, 254)
    scaled = (w * np.exp2(127.0 - byte)[:, None, :]).reshape(k, n).astype(np.float32)
    by_word = np.ascontiguousarray(scaled.reshape(k // 512, 128, 4, n).transpose(0, 1, 3, 2))
    if fmt == "e4m3":
        words = by_word.astype(ml_dtypes.float8_e4m3fn).view(np.uint8)
    else:
        c = by_word.astype(ml_dtypes.float4_e2m1fn).view(np.uint8) & 0xF
        words = c[..., 0::2] | (c[..., 1::2] << 4)
    return np.ascontiguousarray(words), np.ascontiguousarray(byte.astype(np.uint8).reshape(k // 512, 16, n))


def unpack_weight(words, scales, fmt):
    g, p, n, _ = words.shape
    if fmt == "e4m3":
        vals = np.ascontiguousarray(words).view(ml_dtypes.float8_e4m3fn).astype(np.float64)
    else:
        nib = np.empty((g, p, n, 4), np.uint8)
        nib[..., 0::2] = words & 0xF
        nib[..., 1::2] = words >> 4
        vals = E2M1[nib]
    vals = vals * np.repeat(np.exp2(scales.astype(np.float64) - 127.0), 8, axis=1)[..., None]
    return vals.transpose(0, 1, 3, 2).reshape(g * 512, n)
def pack4(w):
    words, scales = pack_weight(w, "e2m1")
    return words.reshape(words.shape[0], 128, -1), scales


def unpack4(words, scales):
    return unpack_weight(words.reshape(words.shape[0], 128, -1, 2), scales, "e2m1")


def planes(Y):
    n, m = Y.shape
    b = f64(bf(Y)).reshape(n // 32, 32, m)
    amax = np.abs(b).max(1)
    byte = np.clip(np.where(amax > 0, np.frexp(amax)[1] - 1 + 127 - 7, 1), 1, 254)
    codes = (b * np.exp2(127.0 - byte)[:, None, :]).reshape(n, m).astype(np.float32).astype(ml_dtypes.float8_e4m3fn).view(np.uint8)
    words = codes.reshape(n // 512, 128, 4, m).transpose(0, 1, 3, 2)
    return np.ascontiguousarray(words), np.ascontiguousarray(byte.astype(np.uint8).reshape(n // 512, 16, m))


M, K, F, N = 1024, 1024, 2048, 1024

def setup_inputs():
    s = mx_kscale(K)
    t = mx_kscale(F)
    x = 0.5 * np.random.randn(K, M)
    x_words, x_scales = pack_weight(x * s[:, None], "e4m3")
    e = (1.2 * np.random.randn(K, F) - 0.8) / np.sqrt(K)
    e_words, e_scales = pack4(e / s[:, None])
    base = np.exp(0.5 * np.random.randn(F))
    size = np.exp(0.8 * np.random.randn(N))
    subst = np.exp(1.5 * np.random.randn(F, N) - 1.125) * size / F
    stock = 1.6 * size * np.exp(0.25 * np.random.randn(N))
    presold = 0.4 * size * np.abs(np.random.randn(M, N))
    return {"x_words": x_words, "x_scales": x_scales, "e_words": e_words, "e_scales": e_scales,
            "base": bf(base * t), "subst": bf(subst / t[:, None]), "stock": bf(stock), "presold": bf(presold)}

def reference(x_words, x_scales, e_words, e_scales, base, subst, stock, presold):
    X = unpack_weight(x_words, x_scales, "e4m3")
    E = unpack4(e_words, e_scales)
    Z = X.T @ E
    Q = f64(base)[None, :] * np.exp(Z)
    U = mxq(Q, 1, "e4m3") @ mxq(f64(subst), 0, "e4m3")
    y = np.minimum(U, f64(stock)[None, :]) + f64(presold)
    Y = y.T
    words, scales = planes(Y)
    return y, words, scales

@@ -1,0 +1,442 @@
+from contextlib import ExitStack
+
+import concourse.mybir as mybir
+from concourse.masks import make_identity
+
+M, K, F, N = 1024, 1024, 2048, 1024
+FLOPS = 2 * M * K * F + 2 * M * F * N
+
+F32 = mybir.dt.float32
+BF16 = mybir.dt.bfloat16
+I32 = mybir.dt.int32
+U32 = mybir.dt.uint32
+U8 = mybir.dt.uint8
+FP8X4 = mybir.dt.float8_e4m3fn_x4
+FP4X4 = mybir.dt.float4_e2m1fn_x4
+ALU = mybir.AluOpType
+ACT = mybir.ActivationFunctionType
+
+P = 128
+W = 512
+KG = K // W
+FG = F // W
+NG = N // W
+MH = M // W
+EZB = 2
+PTB = 6
+YTB = 2
+YRB = 6
+
+
+def tile_capped_substitution_demand_h2_kernel(
+    tc, x_words, x_scales, e_words, e_scales, base, subst, stock, presold, out_0, out_1, out_2
+):
+    nc = tc.nc
+    with ExitStack() as ctx:
+        keep = ctx.enter_context(tc.tile_pool(name="keep", bufs=1))
+        ring = ctx.enter_context(tc.tile_pool(name="ring", bufs=2))
+        psum = ctx.enter_context(tc.psum_pool(name="psum", bufs=4))
+        ctx.enter_context(tc.manual_schedule())
+
+        def kept(name, shape, dtype):
+            return keep.tile(shape, dtype, name=name, align_bytes=64)
+
+        def turning(tag, shape, dtype, bufs):
+            return ring.tile(shape, dtype, name=tag, tag=tag, bufs=bufs, align_bytes=64)
+
+        def bank(tag="quick"):
+            return psum.tile([P, W], F32, name=tag, tag=tag)
+
+        xw = [kept("xw%d" % h, [P, KG, W], U32) for h in range(MH)]
+        xs = kept("xs", [P, KG, M], U8)
+        e_raw = [kept("e_raw%d" % f, [P, KG, W // 2], I32) for f in range(FG)]
+        es_raw = kept("es_raw", [P, KG, F], U8)
+        ew = [kept("ew%d" % f, [P, KG, 2 * W], U8) for f in range(FG)]
+        es = [kept("es%d" % f, [P, KG, W], U8) for f in range(FG)]
+        s_raw = [kept("s_raw%d" % f, [P, 4, N], BF16) for f in range(FG)]
+        pre = [kept("pre%d" % h, [P, 4, N], BF16) for h in range(MH)]
+        ident = kept("ident", [P, P], F32)
+        base_row = kept("base_row", [FG, W], BF16)
+        base_pad = kept("base_pad", [P, 4, P], F32)
+        base_x = kept("base_x", [P, FG, 4, 4], F32)
+        stock_t = kept("stock_t", [P, NG, 4], BF16)
+        warm = kept("warm", [P, 8], F32)
+        y_scales = [kept("y_scales%d" % h, [P, W], U8) for h in range(MH)]
+        stock_wide = kept("stock_wide", [P, N], BF16)
+        capped, y_row, pairs, y_half = {}, {}, {}, {}
+        s_codes, s_scales, q_codes, q_scales = {}, {}, {}, {}
+        ez, q_bf, s_bf, pre_t, u_bank, y_t, y_bf = {}, {}, {}, {}, {}, {}, {}
+
+        def load_x(h):
+            src = x_words.rearrange("g p m t -> p g (m t)")[:, :, 4 * W * h : 4 * W * (h + 1)]
+            nc.sync.dma_start(out=xw[h][:].bitcast(I32), in_=src.bitcast(I32))
+
+        def load_e(f):
+            src = e_words.rearrange("g p b -> p g b")[:, :, 2 * W * f : 2 * W * (f + 1)]
+            nc.sync.dma_start(out=e_raw[f][:], in_=src.bitcast(I32))
+
+        def load_scale_rows(queue, plane, rows, quad):
+            src = rows[:, 4 * quad : 4 * quad + 4, :].rearrange("g r n -> r g n")
+            queue.dma_start(out=plane[32 * quad : 32 * quad + 4, :, :].bitcast(I32), in_=src.bitcast(I32))
+
+        def load_s(f):
+            rows = subst.rearrange("(f q t r) n -> f t q r n", f=FG, t=4, r=8)
+            for t in range(4):
+                nc.sync.dma_start(out=s_raw[f][:, t, :], in_=rows[f, t])
+
+        def load_pre(h):
+            src = presold[W * h : W * (h + 1), :].rearrange("(j p) n -> p j n", p=P)
+            nc.sync.dma_start(out=pre[h][:], in_=src)
+
+        def sort_e(f):
+            nc.vector.tensor_copy(
+                out=ew[f][:].bitcast(I32).rearrange("p g (t q w) -> p g t q w", t=4, w=4),
+                in_=e_raw[f][:].rearrange("p g (q t w) -> p g t q w", t=4, w=4),
+            )
+            nc.vector.tensor_copy(
+                out=es[f][:].bitcast(I32).rearrange("p g (t q w) -> p g t q w", t=4, w=2),
+                in_=es_raw[:, :, W * f : W * (f + 1)].bitcast(I32).rearrange("p g (q t w) -> p g t q w", t=4, w=2),
+            )
+
+        def sort_base():
+            nc.vector.tensor_copy(
+                out=base_pad[0:FG, :, :].rearrange("f t (q r) -> f t q r", r=8),
+                in_=base_row[:].rearrange("f (q t r) -> f t q r", t=4, r=8),
+            )
+
+        def turn_base():
+            acc = bank()
+            for t in range(4):
+                nc.tensor.transpose(acc[:, P * t : P * (t + 1)], base_pad[:, t, :], ident[:])
+            picked = acc[:].rearrange("p (t j) -> p j t", t=4)[:, 0:FG, :]
+            nc.vector.tensor_copy(out=base_x[:], in_=picked.unsqueeze(3).to_broadcast([P, FG, 4, 4]))
+
+        def first(h, f, ts=range(4)):
+            if (h, f) not in ez:
+                ez[h, f] = turning("ez", [P, 4, W], F32, EZB)
+            for t in ts:
+                acc = bank()
+                for g in range(KG):
+                    nc.tensor.matmul_mx(
+                        out=acc[:],
+                        lhsT=ew[f][:, g, 2 * P * t : 2 * P * (t + 1)].bitcast(FP4X4),
+                        lhsT_scale=es[f][:, g, P * t : P * (t + 1)],
+                        rhs=xw[h][:, g, :].bitcast(FP8X4),
+                        rhs_scale=xs[:, g, W * h : W * (h + 1)],
+                        start=(g == 0),
+                        stop=(g == KG - 1),
+                    )
+                nc.scalar.activation(out=ez[h, f][:, t, :], in_=acc[:], func=ACT.Exp)
+
+        def scale_q(h, f):
+            q_bf[h, f] = turning("q_bf", [P, 4 * W], BF16, 2)
+            nc.vector.tensor_tensor(
+                out=q_bf[h, f][:].rearrange("p (c i t) -> p c t i", i=4, t=4),
+                in0=ez[h, f][:].rearrange("p t (c i) -> p c t i", i=4),
+                in1=base_x[:, f, :, :].unsqueeze(1).to_broadcast([P, W // 4, 4, 4]),
+                op=ALU.mult,
+            )
+
+        def quant_q(h, f):
+            q_codes[h, f] = kept("q_codes%d%d" % (h, f), [P, W], U32)
+            q_scales[h, f] = kept("q_scales%d%d" % (h, f), [P, W], U8)
+            nc.vector.quantize_mx(out=q_codes[h, f][:].bitcast(FP8X4), scales=q_scales[h, f][:], in_=q_bf[h, f][:])
+
+        def weave_s(f, g, engine, ts=slice(0, 4)):
+            if (f, g) not in s_bf:
+                s_bf[f, g] = turning("s_bf", [P, 4 * W], BF16, 3)
+            dst = s_bf[f, g][:].rearrange("p (t a b j) -> p t a j b", t=4, b=2, j=4)[:, ts]
+            src = s_raw[f][:, :, W * g : W * (g + 1)].rearrange("p j (a b t) -> p t a j b", b=2, t=4)[:, ts]
+            if engine == "scalar":
+                nc.scalar.copy(out=dst, in_=src)
+            else:
+                nc.vector.tensor_copy(out=dst, in_=src)
+
+        def quant_s(f, g):
+            s_codes[f, g] = kept("s_codes%d%d" % (f, g), [P, W], U32)
+            s_scales[f, g] = kept("s_scales%d%d" % (f, g), [P, W], U8)
+            nc.vector.quantize_mx(out=s_codes[f, g][:].bitcast(FP8X4), scales=s_scales[f, g][:], in_=s_bf[f, g][:])
+
+        def turn_pre(h, g):
+            for u in range(2):
+                acc = bank()
+                for j in range(4):
+                    words = pre[h][:, j, :].bitcast(F32)
+                    nc.tensor.transpose(
+                        acc[:, P * j : P * (j + 1)], words[:, 256 * g + u : 256 * (g + 1) : 2], ident[:]
+                    )
+                pre_t[h, g, u] = turning("pre_t", [P, W], F32, PTB)
+                nc.scalar.copy(out=pre_t[h, g, u][:], in_=acc[:])
+
+        def second(h, g, t, fs=range(FG), tag="held"):
+            if (h, g, t) not in u_bank:
+                u_bank[h, g, t] = bank(tag)
+            for f in fs:
+                nc.tensor.matmul_mx(
+                    out=u_bank[h, g, t][:],
+                    lhsT=s_codes[f, g][:, P * t : P * (t + 1)].bitcast(FP8X4),
+                    lhsT_scale=s_scales[f, g][:, P * t : P * (t + 1)],
+                    rhs=q_codes[h, f][:].bitcast(FP8X4),
+                    rhs_scale=q_scales[h, f][:],
+                    start=(f == 0),
+                    stop=(f == FG - 1),
+                )
+
+        def cap(h, g, t):
+            if (h, g) not in y_t:
+                y_t[h, g] = turning("y_t", [P, 4, W], F32, YTB)
+            nc.vector.scalar_tensor_tensor(
+                out=y_t[h, g][:, t, :],
+                in0=u_bank[h, g, t][:],
+                scalar=stock_t[:, g, t : t + 1],
+                in1=pre_t[h, g, t // 2][:].bitcast(BF16)[:, t % 2 :: 2],
+                op0=ALU.min,
+                op1=ALU.add,
+            )
+
+        def turn_y(h, g, js=range(4), engine="scalar", tag="quick"):
+            for j in js:
+                acc = bank(tag)
+                for t in range(4):
+                    nc.tensor.transpose(acc[:, P * t : P * (t + 1)], y_t[h, g][:, t, P * j : P * (j + 1)], ident[:])
+                y_rows = turning("y_rows", [P, W], F32, YRB)
+                dst = y_rows[:].rearrange("p (n t) -> p n t", t=4)
+                src = acc[:].rearrange("p (t n) -> p n t", t=4)
+                if engine == "scalar":
+                    nc.scalar.copy(out=dst, in_=src)
+                else:
+                    nc.vector.tensor_copy(out=dst, in_=src)
+                m0 = W * h + P * j
+                nc.sync.dma_start(out=out_0[m0 : m0 + P, W * g : W * (g + 1)], in_=y_rows[:])
+
+        def weave_y(h, g, engine="vector"):
+            y_bf[h, g] = turning("y_bf", [P, 4 * W], BF16, 2)
+            dst = y_bf[h, g][:].rearrange("p (c i t) -> p c t i", i=4, t=4)
+            src = y_t[h, g][:].rearrange("p t (c i) -> p c t i", i=4)
+            if engine == "scalar":
+                nc.scalar.copy(out=dst, in_=src)
+            else:
+                nc.vector.tensor_copy(out=dst, in_=src)
+
+        def passes(h, g, f, tag="held"):
+            for t in range(4):
+                second(h, g, t, [f], tag)
+
+        def quant_y(h, g):
+            y_codes = turning("y_codes", [P, W], U32, 4)
+            nc.vector.quantize_mx(
+                out=y_codes[:].bitcast(FP8X4), scales=y_scales[h][4 * g : P, :], in_=y_bf[h, g][:]
+            )
+            dst = out_1[g].rearrange("p m t -> p (m t)")[:, 4 * W * h : 4 * W * (h + 1)]
+            nc.sync.dma_start(out=dst.bitcast(I32), in_=y_codes[:].bitcast(I32))
+
+        def rows_pass(h, g, f, tag="held"):
+            for j in range(4):
+                if (h, g, j) not in u_bank:
+                    u_bank[h, g, j] = bank(tag)
+                rows_mm(h, g, j, f)
+
+        def rows_mm(h, g, j, f):
+            nc.tensor.matmul_mx(
+                out=u_bank[h, g, j][:],
+                lhsT=q_codes[h, f][:, P * j : P * (j + 1)].bitcast(FP8X4),
+                lhsT_scale=q_scales[h, f][:, P * j : P * (j + 1)],
+                rhs=s_codes[f, g][:].bitcast(FP8X4),
+                rhs_scale=s_scales[f, g][:],
+                start=(f == 0),
+                stop=(f == FG - 1),
+            )
+
+        def rows_all(h, g, j, tag="held"):
+            u_bank[h, g, j] = bank(tag)
+            for f in range(FG):
+                rows_mm(h, g, j, f)
+
+        def cols_all(h, g, t, tag="held"):
+            second(h, g, t, range(FG), tag)
+
+        def rows_cap(h, g, j):
+            capped[h, g, j] = turning("capped", [P, W], F32, 2)
+            nc.vector.tensor_tensor(
+                out=capped[h, g, j][:].rearrange("p (n t) -> p n t", t=4),
+                in0=u_bank[h, g, j][:].rearrange("p (t n) -> p n t", t=4),
+                in1=stock_wide[:, W * g : W * (g + 1)].rearrange("p (n t) -> p n t", t=4),
+                op=ALU.min,
+            )
+
+        def rows_add(h, g, j):
+            y_row[h, g, j] = turning("y_rows", [P, W], F32, YRB)
+            nc.vector.tensor_tensor(
+                out=y_row[h, g, j][:], in0=capped[h, g, j][:], in1=pre[h][:, j, W * g : W * (g + 1)], op=ALU.add
+            )
+            m0 = W * h + P * j
+            nc.sync.dma_start(out=out_0[m0 : m0 + P, W * g : W * (g + 1)], in_=y_row[h, g, j][:])
+
+        def rows_sort(h, g, j, engine):
+            pairs[h, g, j] = turning("pairs", [P, W], BF16, 4)
+            dst = pairs[h, g, j][:].rearrange("p (u n e) -> p u n e", u=2, e=2)
+            src = y_row[h, g, j][:].rearrange("p (n u e) -> p u n e", u=2, e=2)
+            if engine == "scalar":
+                nc.scalar.copy(out=dst, in_=src)
+            else:
+                nc.vector.tensor_copy(out=dst, in_=src)
+
+        def rows_turn(h, g, half, tag="quick"):
+            acc = bank(tag)
+            for jj in range(2):
+                for u in range(2):
+                    words = pairs[h, g, 2 * half + jj][:].bitcast(F32)
+                    c0 = P * (2 * jj + u)
+                    nc.tensor.transpose(acc[:, c0 : c0 + P], words[:, P * u : P * (u + 1)], ident[:])
+            y_half[h, g, half] = turning("y_half", [P, 2 * W], BF16, 2)
+            nc.scalar.copy(
+                out=y_half[h, g, half][:].bitcast(F32).rearrange("p (j m u) -> p j m u", j=2, u=2),
+                in_=acc[:].rearrange("p (j u m) -> p j m u", j=2, u=2),
+            )
+
+        def rows_quant(h, g, half):
+            y_codes = turning("y_codes", [P, W], U32, 4)
+            c0 = W // 2 * half
+            nc.vector.quantize_mx(
+                out=y_codes[:, 0 : W // 2].bitcast(FP8X4),
+                scales=y_scales[h][4 * g : P, c0 : c0 + W // 2],
+                in_=y_half[h, g, half][:],
+            )
+            dst = out_1[g].rearrange("p m t -> p (m t)")[:, 4 * (W * h + c0) : 4 * (W * h + c0 + W // 2)]
+            nc.sync.dma_start(out=dst.bitcast(I32), in_=y_codes[:, 0 : W // 2].bitcast(I32))
+
+        def store_scales(h):
+            for quad in range(4):
+                dst = out_2[:, 4 * quad : 4 * quad + 4, W * h : W * (h + 1)]
+                nc.sync.dma_start(out=dst.bitcast(I32), in_=y_scales[h][32 * quad : 32 * quad + 8, :].bitcast(I32))
+
+        def load_stock():
+            nc.sync.dma_start(out=stock_t[:], in_=stock.rearrange("(g p t) -> p g t", g=NG, t=4))
+
+        def load_wide():
+            nc.sync.dma_start(out=stock_wide[:, W:N], in_=stock[W:N].partition_broadcast(P))
+
+        nc.sync.dma_start(out=base_row[:], in_=base.rearrange("(f k) -> f k", f=FG))
+        load_e(0)
+        load_x(0)
+        nc.vector.memset(es_raw[:].bitcast(I32), 0)
+        nc.vector.memset(xs[:].bitcast(I32), 0)
+        nc.vector.memset(warm[:], 0.0)
+        nc.scalar.activation(out=warm[:, 0:1], in_=warm[:, 1:2], func=ACT.Exp)
+        for quad in range(4):
+            load_scale_rows(nc.sync, es_raw, e_scales, quad)
+        for quad in range(4):
+            load_scale_rows(nc.sync if quad < 2 else nc.gpsimd, xs, x_scales, quad)
+        nc.vector.memset(base_pad[:], 0.0)
+        make_identity(nc, ident[:])
+        sort_base()
+        load_e(2)
+        load_e(3)
+        load_e(1)
+        sort_e(0)
+        load_s(0)
+        turn_base()
+        load_s(1)
+        sort_e(2)
+        sort_e(3)
+        first(0, 0)
+        sort_e(1)
+        scale_q(0, 0)
+        first(0, 1)
+        load_pre(0)
+        weave_s(0, 0, "vector")
+        weave_s(1, 0, "vector")
+        load_x(1)
+        weave_s(0, 1, "scalar")
+        first(0, 2)
+        load_s(2)
+        turn_pre(0, 0)
+        scale_q(0, 1)
+        quant_s(0, 0)
+        quant_q(0, 0)
+        quant_q(0, 1)
+        first(0, 3)
+        weave_s(2, 0, "scalar")
+        scale_q(0, 2)
+        scale_q(0, 3)
+        load_pre(1)
+        load_stock()
+        load_s(3)
+        quant_s(0, 1)
+        first(1, 0)
+        turn_pre(0, 1)
+        quant_s(1, 0)
+        quant_s(2, 0)
+        quant_q(0, 2)
+        passes(0, 0, 0, "held")
+        weave_s(3, 0, "vector")
+        quant_s(3, 0)
+        quant_q(0, 3)
+        passes(0, 0, 1)
+        weave_s(3, 1, "scalar")
+        weave_s(2, 1, "vector")
+        passes(0, 0, 2)
+        passes(0, 0, 3)
+        cap(0, 0, 1)
+        cap(0, 0, 0)
+        weave_s(1, 1, "scalar")
+        cap(0, 0, 2)
+        quant_s(2, 1)
+        turn_pre(1, 0)
+        quant_s(1, 1)
+        quant_s(3, 1)
+        cap(0, 0, 3)
+        first(1, 1)
+        cols_all(0, 1, 0, "held")
+        cols_all(0, 1, 1, "held")
+        scale_q(1, 0)
+        cap(0, 1, 1)
+        cap(0, 1, 0)
+        first(1, 2)
+        cols_all(0, 1, 3, "held")
+        scale_q(1, 1)
+        quant_q(1, 1)
+        cols_all(0, 1, 2, "held")
+        first(1, 3)
+        weave_y(0, 0, "vector")
+        turn_y(0, 0, [2,3], "scalar", "quick")
+        cap(0, 1, 3)
+        cap(0, 1, 2)
+        turn_y(0, 1, [2,3], "scalar", "held")
+        turn_y(0, 0, [0,1], "scalar", "quick")
+        turn_pre(1, 1)
+        quant_q(1, 0)
+        scale_q(1, 2)
+        quant_q(1, 2)
+        passes(1, 0, 0, "held")
+        passes(1, 0, 1)
+        scale_q(1, 3)
+        quant_q(1, 3)
+        turn_y(0, 1, [0,1], "scalar", "quick")
+        passes(1, 0, 2)
+        weave_y(0, 1, "scalar")
+        passes(1, 1, 0, "quick")
+        quant_y(0, 0)
+        passes(1, 0, 3)
+        cap(1, 0, 2)
+        passes(1, 1, 1)
+        cap(1, 0, 3)
+        passes(1, 1, 2)
+        quant_y(0, 1)
+        passes(1, 1, 3)
+        cap(1, 0, 0)
+        cap(1, 0, 1)
+        cap(1, 1, 1)
+        cap(1, 1, 2)
+        store_scales(0)
+        cap(1, 1, 0)
+        turn_y(1, 0, [2,3], "scalar", "held")
+        cap(1, 1, 3)
+        weave_y(1, 1, "vector")
+        turn_y(1, 0, [0,1], "scalar", "held")
+        turn_y(1, 1, [2,3], "scalar", "quick")
+        quant_y(1, 1)
+        turn_y(1, 1, [0,1], "scalar", "quick")
+        weave_y(1, 0, "vector")
+        quant_y(1, 0)
+        store_scales(1)

@@ -1,3 +1,4 @@
+import math
 from contextlib import ExitStack
 
 import concourse.mybir as mybir
@@ -22,10 +23,13 @@ KG = K // W
 FG = F // W
 NG = N // W
 MH = M // W
-EZB = 2
-PTB = 6
+EZB = 3
+PTB = 4
 YTB = 2
 YRB = 6
+NATURAL = (1,)
+LN2 = math.log(2.0)
+TINY = 2.0**-126
 
 
 def tile_capped_substitution_demand_h2_kernel(
@@ -58,7 +62,8 @@ def tile_capped_substitution_demand_h2_kernel(
         ident = kept("ident", [P, P], F32)
         base_row = kept("base_row", [FG, W], BF16)
         base_pad = kept("base_pad", [P, 4, P], F32)
-        base_x = kept("base_x", [P, FG, 4, 4], F32)
+        log_b = kept("log_b", [P, 4 * FG], F32)
+        sign_b = kept("sign_b", [P, 4 * FG], F32)
         stock_t = kept("stock_t", [P, NG, 4], BF16)
         warm = kept("warm", [P, 8], F32)
         y_scales = [kept("y_scales%d" % h, [P, W], U8) for h in range(MH)]
@@ -109,11 +114,30 @@ def tile_capped_substitution_demand_h2_kernel(
             for t in range(4):
                 nc.tensor.transpose(acc[:, P * t : P * (t + 1)], base_pad[:, t, :], ident[:])
             picked = acc[:].rearrange("p (t j) -> p j t", t=4)[:, 0:FG, :]
-            nc.vector.tensor_copy(out=base_x[:], in_=picked.unsqueeze(3).to_broadcast([P, FG, 4, 4]))
+            small = [kept("small%d" % i, [P, 4 * FG], F32) for i in range(10)]
+            neg, mag, guess, inv, ratio, d, p0, p1, p2, p3 = [s[:] for s in small]
+            nc.scalar.activation(out=mag.rearrange("p (f t) -> p f t", t=4), in_=picked, func=ACT.Abs)
+            nc.vector.tensor_scalar(
+                out=neg.rearrange("p (f t) -> p f t", t=4), in0=picked, scalar1=0.0, scalar2=-2.0, op0=ALU.is_lt, op1=ALU.mult
+            )
+            nc.vector.tensor_scalar(
+                out=guess, in0=mag.bitcast(I32), scalar1=LN2 / 2**23, scalar2=0.03 - 127 * LN2, op0=ALU.mult, op1=ALU.add
+            )
+            nc.scalar.activation(out=inv, in_=guess, func=ACT.Exp, scale=-1.0)
+            nc.vector.tensor_scalar(out=sign_b[:], in0=neg, scalar1=1.0, scalar2=None, op0=ALU.add)
+            sort_e(0)
+            nc.vector.tensor_tensor(out=ratio, in0=mag, in1=inv, op=ALU.mult)
+            nc.vector.tensor_scalar(out=d, in0=ratio, scalar1=-1.0, scalar2=None, op0=ALU.add)
+            nc.vector.tensor_scalar(out=p0, in0=ratio, scalar1=0.2, scalar2=-0.45, op0=ALU.mult, op1=ALU.add)
+            nc.vector.tensor_tensor(out=p1, in0=p0, in1=d, op=ALU.mult)
+            nc.vector.scalar_tensor_tensor(out=p2, in0=p1, scalar=1.0 / 3.0, in1=d, op0=ALU.add, op1=ALU.mult)
+            nc.vector.scalar_tensor_tensor(out=p3, in0=p2, scalar=-0.5, in1=d, op0=ALU.add, op1=ALU.mult)
+            nc.vector.scalar_tensor_tensor(out=p0, in0=p3, scalar=1.0, in1=d, op0=ALU.add, op1=ALU.mult)
+            nc.vector.tensor_tensor(out=log_b[:], in0=p0, in1=guess, op=ALU.add)
 
         def first(h, f, ts=range(4)):
             if (h, f) not in ez:
-                ez[h, f] = turning("ez", [P, 4, W], F32, EZB)
+                ez[h, f] = turning("ez", [P, 4, W], BF16, EZB)
             for t in ts:
                 acc = bank()
                 for g in range(KG):
@@ -126,16 +150,25 @@ def tile_capped_substitution_demand_h2_kernel(
                         start=(g == 0),
                         stop=(g == KG - 1),
                     )
-                nc.scalar.activation(out=ez[h, f][:, t, :], in_=acc[:], func=ACT.Exp)
+                nc.scalar.activation(
+                    out=ez[h, f][:, t, :], in_=acc[:], func=ACT.Exp, bias=log_b[:, 4 * f + t : 4 * f + t + 1]
+                )
 
-        def scale_q(h, f):
+        def scale_q(h, f, engine="vector"):
             q_bf[h, f] = turning("q_bf", [P, 4 * W], BF16, 2)
-            nc.vector.tensor_tensor(
-                out=q_bf[h, f][:].rearrange("p (c i t) -> p c t i", i=4, t=4),
-                in0=ez[h, f][:].rearrange("p t (c i) -> p c t i", i=4),
-                in1=base_x[:, f, :, :].unsqueeze(1).to_broadcast([P, W // 4, 4, 4]),
-                op=ALU.mult,
-            )
+            dst = q_bf[h, f][:].rearrange("p (c i t) -> p c t i", i=4, t=4)
+            src = ez[h, f][:].rearrange("p t (c i) -> p c t i", i=4)
+            if engine == "scalar":
+                nc.scalar.copy(out=dst, in_=src)
+            else:
+                nc.vector.tensor_copy(out=dst, in_=src)
+
+        def sign_s(f):
+            for t in range(4):
+                row = s_raw[f][:, t, :]
+                nc.vector.tensor_scalar(
+                    out=row, in0=row, scalar1=sign_b[:, 4 * f + t : 4 * f + t + 1], scalar2=None, op0=ALU.mult
+                )
 
         def quant_q(h, f):
             q_codes[h, f] = kept("q_codes%d%d" % (h, f), [P, W], U32)
@@ -147,6 +180,9 @@ def tile_capped_substitution_demand_h2_kernel(
                 s_bf[f, g] = turning("s_bf", [P, 4 * W], BF16, 3)
             dst = s_bf[f, g][:].rearrange("p (t a b j) -> p t a j b", t=4, b=2, j=4)[:, ts]
             src = s_raw[f][:, :, W * g : W * (g + 1)].rearrange("p j (a b t) -> p t a j b", b=2, t=4)[:, ts]
+            if g in NATURAL:
+                dst = s_bf[f, g][:].rearrange("p (c i j) -> p c j i", i=4, j=4)
+                src = s_raw[f][:, :, W * g : W * (g + 1)].rearrange("p j (c i) -> p c j i", i=4)
             if engine == "scalar":
                 nc.scalar.copy(out=dst, in_=src)
             else:
@@ -258,9 +294,9 @@ def tile_capped_substitution_demand_h2_kernel(
         def rows_cap(h, g, j):
             capped[h, g, j] = turning("capped", [P, W], F32, 2)
             nc.vector.tensor_tensor(
-                out=capped[h, g, j][:].rearrange("p (n t) -> p n t", t=4),
-                in0=u_bank[h, g, j][:].rearrange("p (t n) -> p n t", t=4),
-                in1=stock_wide[:, W * g : W * (g + 1)].rearrange("p (n t) -> p n t", t=4),
+                out=capped[h, g, j][:],
+                in0=u_bank[h, g, j][:],
+                in1=stock_wide[:, W * g : W * (g + 1)],
                 op=ALU.min,
             )
 
@@ -314,7 +350,8 @@ def tile_capped_substitution_demand_h2_kernel(
             nc.sync.dma_start(out=stock_t[:], in_=stock.rearrange("(g p t) -> p g t", g=NG, t=4))
 
         def load_wide():
-            nc.sync.dma_start(out=stock_wide[:, W:N], in_=stock[W:N].partition_broadcast(P))
+            lo = W * min(NATURAL)
+            nc.sync.dma_start(out=stock_wide[:, lo:N], in_=stock[lo:N].partition_broadcast(P))
 
         nc.sync.dma_start(out=base_row[:], in_=base.rearrange("(f k) -> f k", f=FG))
         load_e(0)
@@ -323,120 +360,138 @@ def tile_capped_substitution_demand_h2_kernel(
         nc.vector.memset(xs[:].bitcast(I32), 0)
         nc.vector.memset(warm[:], 0.0)
         nc.scalar.activation(out=warm[:, 0:1], in_=warm[:, 1:2], func=ACT.Exp)
+        make_identity(nc, ident[:])
+        nc.vector.memset(base_pad[:], 0.0)
         for quad in range(4):
             load_scale_rows(nc.sync, es_raw, e_scales, quad)
         for quad in range(4):
-            load_scale_rows(nc.sync if quad < 2 else nc.gpsimd, xs, x_scales, quad)
-        nc.vector.memset(base_pad[:], 0.0)
-        make_identity(nc, ident[:])
-        sort_base()
+            load_scale_rows(nc.sync, xs, x_scales, quad)
+        load_e(1)
+        load_s(0)
         load_e(2)
         load_e(3)
-        load_e(1)
-        sort_e(0)
-        load_s(0)
-        turn_base()
         load_s(1)
-        sort_e(2)
-        sort_e(3)
+        load_s(2)
+        load_x(1)
+        load_s(3)
+        load_pre(0)
+        load_stock()
+        load_wide()
+        load_pre(1)
+        sort_base()
+        turn_base()
         first(0, 0)
         sort_e(1)
-        scale_q(0, 0)
         first(0, 1)
-        load_pre(0)
+        sign_s(0)
+        sort_e(2)
         weave_s(0, 0, "vector")
-        weave_s(1, 0, "vector")
-        load_x(1)
         weave_s(0, 1, "scalar")
         first(0, 2)
-        load_s(2)
-        turn_pre(0, 0)
-        scale_q(0, 1)
+        scale_q(0, 0, "vector")
         quant_s(0, 0)
+        sort_e(3)
         quant_q(0, 0)
-        quant_q(0, 1)
-        first(0, 3)
-        weave_s(2, 0, "scalar")
-        scale_q(0, 2)
-        scale_q(0, 3)
-        load_pre(1)
-        load_stock()
-        load_s(3)
+        sign_s(1)
         quant_s(0, 1)
-        first(1, 0)
-        turn_pre(0, 1)
-        quant_s(1, 0)
-        quant_s(2, 0)
-        quant_q(0, 2)
+        weave_s(1, 0, "vector")
+        weave_s(1, 1, "scalar")
+        first(0, 3)
         passes(0, 0, 0, "held")
+        scale_q(0, 1, "vector")
+        quant_s(1, 0)
+        sign_s(2)
+        quant_q(0, 1)
+        weave_s(2, 0, "vector")
+        quant_s(1, 1)
+        weave_s(2, 1, "scalar")
+        first(1, 0)
+        passes(0, 0, 1)
+        scale_q(0, 2, "vector")
+        quant_s(2, 0)
+        sign_s(3)
+        quant_q(0, 2)
         weave_s(3, 0, "vector")
+        quant_s(2, 1)
+        weave_s(3, 1, "scalar")
+        first(1, 1)
+        passes(0, 0, 2)
+        scale_q(0, 3, "vector")
         quant_s(3, 0)
         quant_q(0, 3)
-        passes(0, 0, 1)
-        weave_s(3, 1, "scalar")
-        weave_s(2, 1, "vector")
-        passes(0, 0, 2)
-        passes(0, 0, 3)
-        cap(0, 0, 1)
-        cap(0, 0, 0)
-        weave_s(1, 1, "scalar")
-        cap(0, 0, 2)
-        quant_s(2, 1)
-        turn_pre(1, 0)
-        quant_s(1, 1)
-        quant_s(3, 1)
-        cap(0, 0, 3)
-        first(1, 1)
-        cols_all(0, 1, 0, "held")
-        cols_all(0, 1, 1, "held")
-        scale_q(1, 0)
-        cap(0, 1, 1)
-        cap(0, 1, 0)
+        turn_pre(0, 0)
         first(1, 2)
-        cols_all(0, 1, 3, "held")
-        scale_q(1, 1)
-        quant_q(1, 1)
-        cols_all(0, 1, 2, "held")
-        first(1, 3)
-        weave_y(0, 0, "vector")
-        turn_y(0, 0, [2,3], "scalar", "quick")
-        cap(0, 1, 3)
-        cap(0, 1, 2)
-        turn_y(0, 1, [2,3], "scalar", "held")
-        turn_y(0, 0, [0,1], "scalar", "quick")
-        turn_pre(1, 1)
+        passes(0, 0, 3)
+        scale_q(1, 0, "vector")
+        quant_s(3, 1)
         quant_q(1, 0)
-        scale_q(1, 2)
+        cap(0, 0, 0)
+        cap(0, 0, 1)
+        cap(0, 0, 2)
+        cap(0, 0, 3)
+        first(1, 3)
+        scale_q(1, 1, "vector")
+        rows_all(0, 1, 0, "held")
+        rows_all(0, 1, 1, "held")
+        turn_y(0, 0, [0,1], "scalar", "quick")
+        turn_y(0, 0, [2,3], "scalar", "quick")
+        quant_q(1, 1)
+        scale_q(1, 2, "vector")
+        rows_cap(0, 1, 0)
         quant_q(1, 2)
-        passes(1, 0, 0, "held")
-        passes(1, 0, 1)
-        scale_q(1, 3)
+        rows_add(0, 1, 0)
+        scale_q(1, 3, "vector")
+        weave_y(0, 0, "scalar")
+        rows_all(0, 1, 2, "held")
+        rows_all(0, 1, 3, "held")
+        turn_pre(1, 0)
+        rows_cap(0, 1, 1)
         quant_q(1, 3)
-        turn_y(0, 1, [0,1], "scalar", "quick")
-        passes(1, 0, 2)
-        weave_y(0, 1, "scalar")
-        passes(1, 1, 0, "quick")
+        rows_add(0, 1, 1)
+        rows_sort(0, 1, 0, "scalar")
+        rows_sort(0, 1, 1, "scalar")
+        rows_cap(0, 1, 2)
         quant_y(0, 0)
-        passes(1, 0, 3)
-        cap(1, 0, 2)
-        passes(1, 1, 1)
-        cap(1, 0, 3)
-        passes(1, 1, 2)
-        quant_y(0, 1)
-        passes(1, 1, 3)
+        rows_add(0, 1, 2)
+        cols_all(1, 0, 0, "held")
+        rows_all(1, 1, 0, "held")
+        rows_turn(0, 1, 0, "quick")
+        rows_cap(0, 1, 3)
         cap(1, 0, 0)
+        rows_add(0, 1, 3)
+        rows_sort(0, 1, 2, "scalar")
+        rows_sort(0, 1, 3, "scalar")
+        cols_all(1, 0, 1, "held")
+        rows_all(1, 1, 1, "held")
+        rows_cap(1, 1, 0)
+        rows_quant(0, 1, 0)
+        rows_add(1, 1, 0)
+        rows_turn(0, 1, 1, "quick")
         cap(1, 0, 1)
-        cap(1, 1, 1)
-        cap(1, 1, 2)
+        rows_sort(1, 1, 0, "scalar")
+        cols_all(1, 0, 2, "held")
+        rows_all(1, 1, 2, "held")
+        rows_cap(1, 1, 1)
+        rows_quant(0, 1, 1)
         store_scales(0)
-        cap(1, 1, 0)
-        turn_y(1, 0, [2,3], "scalar", "held")
-        cap(1, 1, 3)
-        weave_y(1, 1, "vector")
-        turn_y(1, 0, [0,1], "scalar", "held")
-        turn_y(1, 1, [2,3], "scalar", "quick")
-        quant_y(1, 1)
-        turn_y(1, 1, [0,1], "scalar", "quick")
+        rows_add(1, 1, 1)
+        cap(1, 0, 2)
+        rows_sort(1, 1, 1, "scalar")
+        cols_all(1, 0, 3, "held")
+        rows_turn(1, 1, 0, "quick")
+        rows_all(1, 1, 3, "held")
+        rows_cap(1, 1, 2)
+        cap(1, 0, 3)
+        rows_add(1, 1, 2)
+        rows_sort(1, 1, 2, "scalar")
+        turn_y(1, 0, [0,1], "scalar", "quick")
+        turn_y(1, 0, [2,3], "scalar", "quick")
+        rows_cap(1, 1, 3)
+        rows_quant(1, 1, 0)
+        rows_add(1, 1, 3)
+        rows_sort(1, 1, 3, "vector")
         weave_y(1, 0, "vector")
+        rows_turn(1, 1, 1, "quick")
         quant_y(1, 0)
+        rows_quant(1, 1, 1)
         store_scales(1)

@@ -18,18 +18,12 @@ ALU = mybir.AluOpType
 ACT = mybir.ActivationFunctionType
 
 P = 128
+SLOTS = 4
 W = 512
-KG = K // W
-FG = F // W
-NG = N // W
-MH = M // W
-EZB = 3
-PTB = 4
-YTB = 2
-YRB = 6
-NATURAL = (1,)
+K_PASSES = K // W
+F_PASSES = F // W
+BY_COLUMNS, BY_ROWS = 0, 1
 LN2 = math.log(2.0)
-TINY = 2.0**-126
 
 
 def tile_capped_substitution_demand_h2_kernel(
@@ -45,327 +39,315 @@ def tile_capped_substitution_demand_h2_kernel(
         def kept(name, shape, dtype):
             return keep.tile(shape, dtype, name=name, align_bytes=64)
 
-        def turning(tag, shape, dtype, bufs):
+        def reused(tag, shape, dtype, bufs):
             return ring.tile(shape, dtype, name=tag, tag=tag, bufs=bufs, align_bytes=64)
 
-        def bank(tag="quick"):
-            return psum.tile([P, W], F32, name=tag, tag=tag)
+        def bank(bank_set):
+            return psum.tile([P, W], F32, name=bank_set, tag=bank_set)
 
-        xw = [kept("xw%d" % h, [P, KG, W], U32) for h in range(MH)]
-        xs = kept("xs", [P, KG, M], U8)
-        e_raw = [kept("e_raw%d" % f, [P, KG, W // 2], I32) for f in range(FG)]
-        es_raw = kept("es_raw", [P, KG, F], U8)
-        ew = [kept("ew%d" % f, [P, KG, 2 * W], U8) for f in range(FG)]
-        es = [kept("es%d" % f, [P, KG, W], U8) for f in range(FG)]
-        s_raw = [kept("s_raw%d" % f, [P, 4, N], BF16) for f in range(FG)]
-        pre = [kept("pre%d" % h, [P, 4, N], BF16) for h in range(MH)]
+        def move(engine, dst, src):
+            if engine == "scalar":
+                nc.scalar.copy(out=dst, in_=src)
+            else:
+                nc.vector.tensor_copy(out=dst, in_=src)
+
+        x_codes = [kept("x_codes%d" % h, [P, K_PASSES, W], U32) for h in range(2)]
+        x_plane = kept("x_plane", [P, K_PASSES, M], U8)
+        e_loaded = [kept("e_loaded%d" % f, [P, K_PASSES, W // 2], I32) for f in range(F_PASSES)]
+        e_plane_loaded = kept("e_plane_loaded", [P, K_PASSES, F], U8)
+        e_codes = [kept("e_codes%d" % f, [P, K_PASSES, 2 * W], U8) for f in range(F_PASSES)]
+        e_plane = [kept("e_plane%d" % f, [P, K_PASSES, W], U8) for f in range(F_PASSES)]
+        s_rows = [kept("s_rows%d" % f, [P, SLOTS, N], BF16) for f in range(F_PASSES)]
+        sold = [kept("sold%d" % h, [P, 4, N], BF16) for h in range(2)]
         ident = kept("ident", [P, P], F32)
-        base_row = kept("base_row", [FG, W], BF16)
-        base_pad = kept("base_pad", [P, 4, P], F32)
-        log_b = kept("log_b", [P, 4 * FG], F32)
-        sign_b = kept("sign_b", [P, 4 * FG], F32)
-        stock_t = kept("stock_t", [P, NG, 4], BF16)
+        base_rows = kept("base_rows", [F_PASSES, W], BF16)
+        base_padded = kept("base_padded", [P, SLOTS, P], F32)
+        log_base = kept("log_base", [P, F_PASSES * SLOTS], F32)
+        sign_base = kept("sign_base", [P, F_PASSES * SLOTS], F32)
+        stock_down = kept("stock_down", [P, 2, SLOTS], BF16)
         warm = kept("warm", [P, 8], F32)
-        y_scales = [kept("y_scales%d" % h, [P, W], U8) for h in range(MH)]
-        stock_wide = kept("stock_wide", [P, N], BF16)
-        capped, y_row, pairs, y_half = {}, {}, {}, {}
-        s_codes, s_scales, q_codes, q_scales = {}, {}, {}, {}
-        ez, q_bf, s_bf, pre_t, u_bank, y_t, y_bf = {}, {}, {}, {}, {}, {}, {}
+        y_plane = kept("y_plane", [P, M], U8)
+        stock_across = kept("stock_across", [P, W], BF16)
+        s_codes, s_plane, q_codes, q_plane = {}, {}, {}, {}
+        q_slots, q_woven, s_woven, sold_turned, u_bank, y_columns, y_woven = {}, {}, {}, {}, {}, {}, {}
+        capped, y_rows, y_pairs = {}, {}, {}
+
+        def load_scale_rows(plane, rows):
+            for quad in range(4):
+                src = rows[:, 4 * quad : 4 * quad + 4, :].rearrange("g r n -> r g n")
+                nc.sync.dma_start(out=plane[32 * quad : 32 * quad + 4, :, :].bitcast(I32), in_=src.bitcast(I32))
 
         def load_x(h):
-            src = x_words.rearrange("g p m t -> p g (m t)")[:, :, 4 * W * h : 4 * W * (h + 1)]
-            nc.sync.dma_start(out=xw[h][:].bitcast(I32), in_=src.bitcast(I32))
+            src = x_words.rearrange("g p m t -> p g (m t)")[:, :, SLOTS * W * h : SLOTS * W * (h + 1)]
+            nc.sync.dma_start(out=x_codes[h][:].bitcast(I32), in_=src.bitcast(I32))
 
         def load_e(f):
             src = e_words.rearrange("g p b -> p g b")[:, :, 2 * W * f : 2 * W * (f + 1)]
-            nc.sync.dma_start(out=e_raw[f][:], in_=src.bitcast(I32))
-
-        def load_scale_rows(queue, plane, rows, quad):
-            src = rows[:, 4 * quad : 4 * quad + 4, :].rearrange("g r n -> r g n")
-            queue.dma_start(out=plane[32 * quad : 32 * quad + 4, :, :].bitcast(I32), in_=src.bitcast(I32))
+            nc.sync.dma_start(out=e_loaded[f][:], in_=src.bitcast(I32))
 
         def load_s(f):
-            rows = subst.rearrange("(f q t r) n -> f t q r n", f=FG, t=4, r=8)
-            for t in range(4):
-                nc.sync.dma_start(out=s_raw[f][:, t, :], in_=rows[f, t])
+            rows = subst.rearrange("(f q t r) n -> f t q r n", f=F_PASSES, t=SLOTS, r=8)
+            for t in range(SLOTS):
+                nc.sync.dma_start(out=s_rows[f][:, t, :], in_=rows[f, t])
 
-        def load_pre(h):
+        def load_sold(h):
             src = presold[W * h : W * (h + 1), :].rearrange("(j p) n -> p j n", p=P)
-            nc.sync.dma_start(out=pre[h][:], in_=src)
+            nc.sync.dma_start(out=sold[h][:], in_=src)
 
         def sort_e(f):
             nc.vector.tensor_copy(
-                out=ew[f][:].bitcast(I32).rearrange("p g (t q w) -> p g t q w", t=4, w=4),
-                in_=e_raw[f][:].rearrange("p g (q t w) -> p g t q w", t=4, w=4),
+                out=e_codes[f][:].bitcast(I32).rearrange("p g (t q w) -> p g t q w", t=SLOTS, w=4),
+                in_=e_loaded[f][:].rearrange("p g (q t w) -> p g t q w", t=SLOTS, w=4),
             )
+            loaded = e_plane_loaded[:, :, W * f : W * (f + 1)].bitcast(I32)
             nc.vector.tensor_copy(
-                out=es[f][:].bitcast(I32).rearrange("p g (t q w) -> p g t q w", t=4, w=2),
-                in_=es_raw[:, :, W * f : W * (f + 1)].bitcast(I32).rearrange("p g (q t w) -> p g t q w", t=4, w=2),
+                out=e_plane[f][:].bitcast(I32).rearrange("p g (t q w) -> p g t q w", t=SLOTS, w=2),
+                in_=loaded.rearrange("p g (q t w) -> p g t q w", t=SLOTS, w=2),
             )
 
-        def sort_base():
+        def prepare_base():
             nc.vector.tensor_copy(
-                out=base_pad[0:FG, :, :].rearrange("f t (q r) -> f t q r", r=8),
-                in_=base_row[:].rearrange("f (q t r) -> f t q r", t=4, r=8),
+                out=base_padded[0:F_PASSES, :, :].rearrange("f t (q r) -> f t q r", r=8),
+                in_=base_rows[:].rearrange("f (q t r) -> f t q r", t=SLOTS, r=8),
             )
-
-        def turn_base():
-            acc = bank()
-            for t in range(4):
-                nc.tensor.transpose(acc[:, P * t : P * (t + 1)], base_pad[:, t, :], ident[:])
-            picked = acc[:].rearrange("p (t j) -> p j t", t=4)[:, 0:FG, :]
-            small = [kept("small%d" % i, [P, 4 * FG], F32) for i in range(10)]
-            neg, mag, guess, inv, ratio, d, p0, p1, p2, p3 = [s[:] for s in small]
-            nc.scalar.activation(out=mag.rearrange("p (f t) -> p f t", t=4), in_=picked, func=ACT.Abs)
+            acc = bank("short")
+            for t in range(SLOTS):
+                nc.tensor.transpose(acc[:, P * t : P * (t + 1)], base_padded[:, t, :], ident[:])
+            values = acc[:].rearrange("p (t f) -> p f t", t=SLOTS)[:, 0:F_PASSES, :]
+            small = [kept("small%d" % i, [P, F_PASSES * SLOTS], F32) for i in range(10)]
+            negative, size, guess, inverse, ratio, d, p0, p1, p2, p3 = [tile[:] for tile in small]
+            nc.scalar.activation(out=size.rearrange("p (f t) -> p f t", t=SLOTS), in_=values, func=ACT.Abs)
             nc.vector.tensor_scalar(
-                out=neg.rearrange("p (f t) -> p f t", t=4), in0=picked, scalar1=0.0, scalar2=-2.0, op0=ALU.is_lt, op1=ALU.mult
+                out=negative.rearrange("p (f t) -> p f t", t=SLOTS),
+                in0=values,
+                scalar1=0.0,
+                scalar2=-2.0,
+                op0=ALU.is_lt,
+                op1=ALU.mult,
             )
             nc.vector.tensor_scalar(
-                out=guess, in0=mag.bitcast(I32), scalar1=LN2 / 2**23, scalar2=0.03 - 127 * LN2, op0=ALU.mult, op1=ALU.add
+                out=guess,
+                in0=size.bitcast(I32),
+                scalar1=LN2 / 2**23,
+                scalar2=0.03 - 127 * LN2,
+                op0=ALU.mult,
+                op1=ALU.add,
             )
-            nc.scalar.activation(out=inv, in_=guess, func=ACT.Exp, scale=-1.0)
-            nc.vector.tensor_scalar(out=sign_b[:], in0=neg, scalar1=1.0, scalar2=None, op0=ALU.add)
-            sort_e(0)
-            nc.vector.tensor_tensor(out=ratio, in0=mag, in1=inv, op=ALU.mult)
+            nc.scalar.activation(out=inverse, in_=guess, func=ACT.Exp, scale=-1.0)
+            nc.vector.tensor_scalar(out=sign_base[:], in0=negative, scalar1=1.0, scalar2=None, op0=ALU.add)
+            nc.vector.tensor_tensor(out=ratio, in0=size, in1=inverse, op=ALU.mult)
             nc.vector.tensor_scalar(out=d, in0=ratio, scalar1=-1.0, scalar2=None, op0=ALU.add)
-            nc.vector.tensor_scalar(out=p0, in0=ratio, scalar1=0.2, scalar2=-0.45, op0=ALU.mult, op1=ALU.add)
+            nc.vector.tensor_scalar(out=p0, in0=ratio, scalar1=0.2, scalar2=-0.2 - 0.25, op0=ALU.mult, op1=ALU.add)
             nc.vector.tensor_tensor(out=p1, in0=p0, in1=d, op=ALU.mult)
+            sort_e(0)
             nc.vector.scalar_tensor_tensor(out=p2, in0=p1, scalar=1.0 / 3.0, in1=d, op0=ALU.add, op1=ALU.mult)
             nc.vector.scalar_tensor_tensor(out=p3, in0=p2, scalar=-0.5, in1=d, op0=ALU.add, op1=ALU.mult)
             nc.vector.scalar_tensor_tensor(out=p0, in0=p3, scalar=1.0, in1=d, op0=ALU.add, op1=ALU.mult)
-            nc.vector.tensor_tensor(out=log_b[:], in0=p0, in1=guess, op=ALU.add)
+            nc.vector.tensor_tensor(out=log_base[:], in0=p0, in1=guess, op=ALU.add)
 
-        def first(h, f, ts=range(4)):
-            if (h, f) not in ez:
-                ez[h, f] = turning("ez", [P, 4, W], BF16, EZB)
-            for t in ts:
-                acc = bank()
-                for g in range(KG):
+        def demand(h, f):
+            q_slots[h, f] = reused("q_slots", [P, SLOTS, W], BF16, 4)
+            for t in range(SLOTS):
+                acc = bank("short")
+                for g in range(K_PASSES):
                     nc.tensor.matmul_mx(
                         out=acc[:],
-                        lhsT=ew[f][:, g, 2 * P * t : 2 * P * (t + 1)].bitcast(FP4X4),
-                        lhsT_scale=es[f][:, g, P * t : P * (t + 1)],
-                        rhs=xw[h][:, g, :].bitcast(FP8X4),
-                        rhs_scale=xs[:, g, W * h : W * (h + 1)],
+                        lhsT=e_codes[f][:, g, 2 * P * t : 2 * P * (t + 1)].bitcast(FP4X4),
+                        lhsT_scale=e_plane[f][:, g, P * t : P * (t + 1)],
+                        rhs=x_codes[h][:, g, :].bitcast(FP8X4),
+                        rhs_scale=x_plane[:, g, W * h : W * (h + 1)],
                         start=(g == 0),
-                        stop=(g == KG - 1),
+                        stop=(g == K_PASSES - 1),
                     )
+                column = SLOTS * f + t
                 nc.scalar.activation(
-                    out=ez[h, f][:, t, :], in_=acc[:], func=ACT.Exp, bias=log_b[:, 4 * f + t : 4 * f + t + 1]
+                    out=q_slots[h, f][:, t, :], in_=acc[:], func=ACT.Exp, bias=log_base[:, column : column + 1]
                 )
 
-        def scale_q(h, f, engine="vector"):
-            q_bf[h, f] = turning("q_bf", [P, 4 * W], BF16, 2)
-            dst = q_bf[h, f][:].rearrange("p (c i t) -> p c t i", i=4, t=4)
-            src = ez[h, f][:].rearrange("p t (c i) -> p c t i", i=4)
-            if engine == "scalar":
-                nc.scalar.copy(out=dst, in_=src)
-            else:
-                nc.vector.tensor_copy(out=dst, in_=src)
+        def weave(engine, dst, src):
+            move(
+                engine,
+                dst.rearrange("p (c i t) -> p c t i", i=4, t=SLOTS),
+                src.rearrange("p t (c i) -> p c t i", i=4),
+            )
+
+        def weave_q(h, f, engine):
+            q_woven[h, f] = reused("q_woven", [P, SLOTS * W], BF16, 3)
+            weave(engine, q_woven[h, f][:], q_slots[h, f][:])
+
+        def quantise_q(h, f):
+            q_codes[h, f] = kept("q_codes%d%d" % (h, f), [P, W], U32)
+            q_plane[h, f] = kept("q_plane%d%d" % (h, f), [P, W], U8)
+            nc.vector.quantize_mx(out=q_codes[h, f][:].bitcast(FP8X4), scales=q_plane[h, f][:], in_=q_woven[h, f][:])
 
         def sign_s(f):
-            for t in range(4):
-                row = s_raw[f][:, t, :]
+            for t in range(SLOTS):
+                row = s_rows[f][:, t, :]
+                column = SLOTS * f + t
                 nc.vector.tensor_scalar(
-                    out=row, in0=row, scalar1=sign_b[:, 4 * f + t : 4 * f + t + 1], scalar2=None, op0=ALU.mult
+                    out=row, in0=row, scalar1=sign_base[:, column : column + 1], scalar2=None, op0=ALU.mult
                 )
 
-        def quant_q(h, f):
-            q_codes[h, f] = kept("q_codes%d%d" % (h, f), [P, W], U32)
-            q_scales[h, f] = kept("q_scales%d%d" % (h, f), [P, W], U8)
-            nc.vector.quantize_mx(out=q_codes[h, f][:].bitcast(FP8X4), scales=q_scales[h, f][:], in_=q_bf[h, f][:])
-
-        def weave_s(f, g, engine, ts=slice(0, 4)):
-            if (f, g) not in s_bf:
-                s_bf[f, g] = turning("s_bf", [P, 4 * W], BF16, 3)
-            dst = s_bf[f, g][:].rearrange("p (t a b j) -> p t a j b", t=4, b=2, j=4)[:, ts]
-            src = s_raw[f][:, :, W * g : W * (g + 1)].rearrange("p j (a b t) -> p t a j b", b=2, t=4)[:, ts]
-            if g in NATURAL:
-                dst = s_bf[f, g][:].rearrange("p (c i j) -> p c j i", i=4, j=4)
-                src = s_raw[f][:, :, W * g : W * (g + 1)].rearrange("p j (c i) -> p c j i", i=4)
-            if engine == "scalar":
-                nc.scalar.copy(out=dst, in_=src)
+        def weave_s(f, g, engine):
+            s_woven[f, g] = reused("s_woven", [P, SLOTS * W], BF16, 3)
+            src = s_rows[f][:, :, W * g : W * (g + 1)]
+            if g == BY_ROWS:
+                weave(engine, s_woven[f, g][:], src)
             else:
-                nc.vector.tensor_copy(out=dst, in_=src)
+                move(
+                    engine,
+                    s_woven[f, g][:].rearrange("p (u a b t) -> p u a t b", u=SLOTS, b=2, t=SLOTS),
+                    src.rearrange("p t (a b u) -> p u a t b", b=2, u=SLOTS),
+                )
 
-        def quant_s(f, g):
+        def quantise_s(f, g):
             s_codes[f, g] = kept("s_codes%d%d" % (f, g), [P, W], U32)
-            s_scales[f, g] = kept("s_scales%d%d" % (f, g), [P, W], U8)
-            nc.vector.quantize_mx(out=s_codes[f, g][:].bitcast(FP8X4), scales=s_scales[f, g][:], in_=s_bf[f, g][:])
+            s_plane[f, g] = kept("s_plane%d%d" % (f, g), [P, W], U8)
+            nc.vector.quantize_mx(out=s_codes[f, g][:].bitcast(FP8X4), scales=s_plane[f, g][:], in_=s_woven[f, g][:])
 
-        def turn_pre(h, g):
-            for u in range(2):
-                acc = bank()
-                for j in range(4):
-                    words = pre[h][:, j, :].bitcast(F32)
-                    nc.tensor.transpose(
-                        acc[:, P * j : P * (j + 1)], words[:, 256 * g + u : 256 * (g + 1) : 2], ident[:]
-                    )
-                pre_t[h, g, u] = turning("pre_t", [P, W], F32, PTB)
-                nc.scalar.copy(out=pre_t[h, g, u][:], in_=acc[:])
+        def store_rows(h, g, pair):
+            m0 = W * h + 2 * P * pair
+            dst = out_0[m0 : m0 + 2 * P, W * g : W * (g + 1)].rearrange("(j p) n -> p j n", p=P)
+            nc.sync.dma_start(out=dst, in_=y_rows[h, g, pair][:])
 
-        def second(h, g, t, fs=range(FG), tag="held"):
-            if (h, g, t) not in u_bank:
-                u_bank[h, g, t] = bank(tag)
-            for f in fs:
-                nc.tensor.matmul_mx(
-                    out=u_bank[h, g, t][:],
-                    lhsT=s_codes[f, g][:, P * t : P * (t + 1)].bitcast(FP8X4),
-                    lhsT_scale=s_scales[f, g][:, P * t : P * (t + 1)],
-                    rhs=q_codes[h, f][:].bitcast(FP8X4),
-                    rhs_scale=q_scales[h, f][:],
-                    start=(f == 0),
-                    stop=(f == FG - 1),
-                )
-
-        def cap(h, g, t):
-            if (h, g) not in y_t:
-                y_t[h, g] = turning("y_t", [P, 4, W], F32, YTB)
-            nc.vector.scalar_tensor_tensor(
-                out=y_t[h, g][:, t, :],
-                in0=u_bank[h, g, t][:],
-                scalar=stock_t[:, g, t : t + 1],
-                in1=pre_t[h, g, t // 2][:].bitcast(BF16)[:, t % 2 :: 2],
-                op0=ALU.min,
-                op1=ALU.add,
-            )
-
-        def turn_y(h, g, js=range(4), engine="scalar", tag="quick"):
-            for j in js:
-                acc = bank(tag)
-                for t in range(4):
-                    nc.tensor.transpose(acc[:, P * t : P * (t + 1)], y_t[h, g][:, t, P * j : P * (j + 1)], ident[:])
-                y_rows = turning("y_rows", [P, W], F32, YRB)
-                dst = y_rows[:].rearrange("p (n t) -> p n t", t=4)
-                src = acc[:].rearrange("p (t n) -> p n t", t=4)
-                if engine == "scalar":
-                    nc.scalar.copy(out=dst, in_=src)
-                else:
-                    nc.vector.tensor_copy(out=dst, in_=src)
-                m0 = W * h + P * j
-                nc.sync.dma_start(out=out_0[m0 : m0 + P, W * g : W * (g + 1)], in_=y_rows[:])
-
-        def weave_y(h, g, engine="vector"):
-            y_bf[h, g] = turning("y_bf", [P, 4 * W], BF16, 2)
-            dst = y_bf[h, g][:].rearrange("p (c i t) -> p c t i", i=4, t=4)
-            src = y_t[h, g][:].rearrange("p t (c i) -> p c t i", i=4)
-            if engine == "scalar":
-                nc.scalar.copy(out=dst, in_=src)
-            else:
-                nc.vector.tensor_copy(out=dst, in_=src)
-
-        def passes(h, g, f, tag="held"):
-            for t in range(4):
-                second(h, g, t, [f], tag)
-
-        def quant_y(h, g):
-            y_codes = turning("y_codes", [P, W], U32, 4)
+        def quantise_y(h, g):
+            y_codes = reused("y_codes", [P, W], U32, 3)
             nc.vector.quantize_mx(
-                out=y_codes[:].bitcast(FP8X4), scales=y_scales[h][4 * g : P, :], in_=y_bf[h, g][:]
+                out=y_codes[:].bitcast(FP8X4), scales=y_plane[4 * g : P, W * h : W * (h + 1)], in_=y_woven[h, g][:]
             )
-            dst = out_1[g].rearrange("p m t -> p (m t)")[:, 4 * W * h : 4 * W * (h + 1)]
+            dst = out_1[g].rearrange("p m t -> p (m t)")[:, SLOTS * W * h : SLOTS * W * (h + 1)]
             nc.sync.dma_start(out=dst.bitcast(I32), in_=y_codes[:].bitcast(I32))
 
-        def rows_pass(h, g, f, tag="held"):
-            for j in range(4):
-                if (h, g, j) not in u_bank:
-                    u_bank[h, g, j] = bank(tag)
-                rows_mm(h, g, j, f)
-
-        def rows_mm(h, g, j, f):
-            nc.tensor.matmul_mx(
-                out=u_bank[h, g, j][:],
-                lhsT=q_codes[h, f][:, P * j : P * (j + 1)].bitcast(FP8X4),
-                lhsT_scale=q_scales[h, f][:, P * j : P * (j + 1)],
-                rhs=s_codes[f, g][:].bitcast(FP8X4),
-                rhs_scale=s_scales[f, g][:],
-                start=(f == 0),
-                stop=(f == FG - 1),
-            )
-
-        def rows_all(h, g, j, tag="held"):
-            u_bank[h, g, j] = bank(tag)
-            for f in range(FG):
-                rows_mm(h, g, j, f)
-
-        def cols_all(h, g, t, tag="held"):
-            second(h, g, t, range(FG), tag)
-
-        def rows_cap(h, g, j):
-            capped[h, g, j] = turning("capped", [P, W], F32, 2)
-            nc.vector.tensor_tensor(
-                out=capped[h, g, j][:],
-                in0=u_bank[h, g, j][:],
-                in1=stock_wide[:, W * g : W * (g + 1)],
-                op=ALU.min,
-            )
-
-        def rows_add(h, g, j):
-            y_row[h, g, j] = turning("y_rows", [P, W], F32, YRB)
-            nc.vector.tensor_tensor(
-                out=y_row[h, g, j][:], in0=capped[h, g, j][:], in1=pre[h][:, j, W * g : W * (g + 1)], op=ALU.add
-            )
-            m0 = W * h + P * j
-            nc.sync.dma_start(out=out_0[m0 : m0 + P, W * g : W * (g + 1)], in_=y_row[h, g, j][:])
-
-        def rows_sort(h, g, j, engine):
-            pairs[h, g, j] = turning("pairs", [P, W], BF16, 4)
-            dst = pairs[h, g, j][:].rearrange("p (u n e) -> p u n e", u=2, e=2)
-            src = y_row[h, g, j][:].rearrange("p (n u e) -> p u n e", u=2, e=2)
-            if engine == "scalar":
-                nc.scalar.copy(out=dst, in_=src)
-            else:
-                nc.vector.tensor_copy(out=dst, in_=src)
-
-        def rows_turn(h, g, half, tag="quick"):
-            acc = bank(tag)
-            for jj in range(2):
-                for u in range(2):
-                    words = pairs[h, g, 2 * half + jj][:].bitcast(F32)
-                    c0 = P * (2 * jj + u)
-                    nc.tensor.transpose(acc[:, c0 : c0 + P], words[:, P * u : P * (u + 1)], ident[:])
-            y_half[h, g, half] = turning("y_half", [P, 2 * W], BF16, 2)
-            nc.scalar.copy(
-                out=y_half[h, g, half][:].bitcast(F32).rearrange("p (j m u) -> p j m u", j=2, u=2),
-                in_=acc[:].rearrange("p (j u m) -> p j m u", j=2, u=2),
-            )
-
-        def rows_quant(h, g, half):
-            y_codes = turning("y_codes", [P, W], U32, 4)
-            c0 = W // 2 * half
-            nc.vector.quantize_mx(
-                out=y_codes[:, 0 : W // 2].bitcast(FP8X4),
-                scales=y_scales[h][4 * g : P, c0 : c0 + W // 2],
-                in_=y_half[h, g, half][:],
-            )
-            dst = out_1[g].rearrange("p m t -> p (m t)")[:, 4 * (W * h + c0) : 4 * (W * h + c0 + W // 2)]
-            nc.sync.dma_start(out=dst.bitcast(I32), in_=y_codes[:, 0 : W // 2].bitcast(I32))
-
-        def store_scales(h):
+        def store_plane():
             for quad in range(4):
-                dst = out_2[:, 4 * quad : 4 * quad + 4, W * h : W * (h + 1)]
-                nc.sync.dma_start(out=dst.bitcast(I32), in_=y_scales[h][32 * quad : 32 * quad + 8, :].bitcast(I32))
+                dst = out_2[:, 4 * quad : 4 * quad + 4, :]
+                nc.sync.dma_start(out=dst.bitcast(I32), in_=y_plane[32 * quad : 32 * quad + 8, :].bitcast(I32))
 
-        def load_stock():
-            nc.sync.dma_start(out=stock_t[:], in_=stock.rearrange("(g p t) -> p g t", g=NG, t=4))
+        def column_pass(h, t, f):
+            nc.tensor.matmul_mx(
+                out=u_bank[h, BY_COLUMNS, t][:],
+                lhsT=s_codes[f, BY_COLUMNS][:, P * t : P * (t + 1)].bitcast(FP8X4),
+                lhsT_scale=s_plane[f, BY_COLUMNS][:, P * t : P * (t + 1)],
+                rhs=q_codes[h, f][:].bitcast(FP8X4),
+                rhs_scale=q_plane[h, f][:],
+                start=(f == 0),
+                stop=(f == F_PASSES - 1),
+            )
 
-        def load_wide():
-            lo = W * min(NATURAL)
-            nc.sync.dma_start(out=stock_wide[:, lo:N], in_=stock[lo:N].partition_broadcast(P))
+        def column_passes_of_streams(h, f):
+            for t in range(SLOTS):
+                if f == 0:
+                    u_bank[h, BY_COLUMNS, t] = bank("long")
+                column_pass(h, t, f)
 
-        nc.sync.dma_start(out=base_row[:], in_=base.rearrange("(f k) -> f k", f=FG))
-        load_e(0)
-        load_x(0)
-        nc.vector.memset(es_raw[:].bitcast(I32), 0)
-        nc.vector.memset(xs[:].bitcast(I32), 0)
+        def column_bank(h, t, bank_set):
+            u_bank[h, BY_COLUMNS, t] = bank(bank_set)
+            for f in range(F_PASSES):
+                column_pass(h, t, f)
+
+        def turn_sold(h):
+            for u in range(2):
+                acc = bank("short")
+                for j in range(4):
+                    words = sold[h][:, j, :].bitcast(F32)
+                    nc.tensor.transpose(acc[:, P * j : P * (j + 1)], words[:, u : W // 2 : 2], ident[:])
+                sold_turned[h, u] = reused("sold_turned", [P, W], F32, 4)
+                nc.scalar.copy(out=sold_turned[h, u][:], in_=acc[:])
+
+        def finish_columns(h):
+            y_columns[h] = reused("y_columns", [P, SLOTS, W], F32, 2)
+            for t in range(SLOTS):
+                nc.vector.scalar_tensor_tensor(
+                    out=y_columns[h][:, t, :],
+                    in0=u_bank[h, BY_COLUMNS, t][:],
+                    scalar=stock_down[:, BY_COLUMNS, t : t + 1],
+                    in1=sold_turned[h, t // 2][:].bitcast(BF16)[:, t % 2 :: 2],
+                    op0=ALU.min,
+                    op1=ALU.add,
+                )
+
+        def turn_columns(h, pair, bank_set):
+            y_rows[h, BY_COLUMNS, pair] = reused("y_rows", [P, 2, W], F32, 4)
+            for i in range(2):
+                j = 2 * pair + i
+                acc = bank(bank_set)
+                for t in range(SLOTS):
+                    nc.tensor.transpose(acc[:, P * t : P * (t + 1)], y_columns[h][:, t, P * j : P * (j + 1)], ident[:])
+                nc.scalar.copy(
+                    out=y_rows[h, BY_COLUMNS, pair][:, i, :].rearrange("p (n t) -> p n t", t=SLOTS),
+                    in_=acc[:].rearrange("p (t n) -> p n t", t=SLOTS),
+                )
+            store_rows(h, BY_COLUMNS, pair)
+
+        def weave_columns(h, engine):
+            y_woven[h, BY_COLUMNS] = reused("y_woven", [P, SLOTS * W], BF16, 2)
+            weave(engine, y_woven[h, BY_COLUMNS][:], y_columns[h][:])
+
+        def row_bank(h, j, bank_set):
+            u_bank[h, BY_ROWS, j] = bank(bank_set)
+            for f in range(F_PASSES):
+                nc.tensor.matmul_mx(
+                    out=u_bank[h, BY_ROWS, j][:],
+                    lhsT=q_codes[h, f][:, P * j : P * (j + 1)].bitcast(FP8X4),
+                    lhsT_scale=q_plane[h, f][:, P * j : P * (j + 1)],
+                    rhs=s_codes[f, BY_ROWS][:].bitcast(FP8X4),
+                    rhs_scale=s_plane[f, BY_ROWS][:],
+                    start=(f == 0),
+                    stop=(f == F_PASSES - 1),
+                )
+
+        def cap_rows(h, pair):
+            for j in (2 * pair, 2 * pair + 1):
+                capped[h, j] = reused("capped", [P, W], F32, 2)
+                nc.vector.tensor_tensor(
+                    out=capped[h, j][:], in0=u_bank[h, BY_ROWS, j][:], in1=stock_across[:], op=ALU.min
+                )
+
+        def add_rows(h, pair):
+            y_rows[h, BY_ROWS, pair] = reused("y_rows", [P, 2, W], F32, 4)
+            for i in range(2):
+                j = 2 * pair + i
+                nc.vector.tensor_tensor(
+                    out=y_rows[h, BY_ROWS, pair][:, i, :], in0=capped[h, j][:], in1=sold[h][:, j, W:N], op=ALU.add
+                )
+            store_rows(h, BY_ROWS, pair)
+
+        def round_rows(h):
+            for j in range(4):
+                y_pairs[h, j] = reused("y_pairs", [P, W], BF16, 4)
+                nc.scalar.copy(
+                    out=y_pairs[h, j][:].rearrange("p (u n e) -> p u n e", u=2, e=2),
+                    in_=y_rows[h, BY_ROWS, j // 2][:, j % 2, :].rearrange("p (n u e) -> p u n e", u=2, e=2),
+                )
+
+        def turn_rows(h, bank_set):
+            y_woven[h, BY_ROWS] = reused("y_woven", [P, SLOTS * W], BF16, 2)
+            for pair in range(2):
+                acc = bank(bank_set)
+                for i in range(2):
+                    words = y_pairs[h, 2 * pair + i][:].bitcast(F32)
+                    for u in range(2):
+                        c0 = P * (2 * i + u)
+                        nc.tensor.transpose(acc[:, c0 : c0 + P], words[:, P * u : P * (u + 1)], ident[:])
+                dst = y_woven[h, BY_ROWS][:, 2 * W * pair : 2 * W * (pair + 1)].bitcast(F32)
+                nc.scalar.copy(
+                    out=dst.rearrange("p (i m u) -> p i m u", i=2, u=2),
+                    in_=acc[:].rearrange("p (i u m) -> p i m u", i=2, u=2),
+                )
+
+        nc.gpsimd.memset(x_plane[:].bitcast(I32), 0)
+        nc.vector.memset(e_plane_loaded[:].bitcast(I32), 0)
+        nc.vector.memset(ident[:], 0.0)
         nc.vector.memset(warm[:], 0.0)
         nc.scalar.activation(out=warm[:, 0:1], in_=warm[:, 1:2], func=ACT.Exp)
-        make_identity(nc, ident[:])
-        nc.vector.memset(base_pad[:], 0.0)
-        for quad in range(4):
-            load_scale_rows(nc.sync, es_raw, e_scales, quad)
-        for quad in range(4):
-            load_scale_rows(nc.sync, xs, x_scales, quad)
+        make_identity(nc, ident[:], nomemset=True)
+        nc.vector.memset(base_padded[:], 0.0)
+
+        nc.sync.dma_start(out=base_rows[:], in_=base.rearrange("(f k) -> f k", f=F_PASSES))
+        load_scale_rows(x_plane, x_scales)
+        load_scale_rows(e_plane_loaded, e_scales)
+        load_e(0)
+        load_x(0)
         load_e(1)
         load_s(0)
         load_e(2)
@@ -374,124 +356,88 @@ def tile_capped_substitution_demand_h2_kernel(
         load_s(2)
         load_x(1)
         load_s(3)
-        load_pre(0)
-        load_stock()
-        load_wide()
-        load_pre(1)
-        sort_base()
-        turn_base()
-        first(0, 0)
+        load_sold(0)
+        nc.sync.dma_start(out=stock_down[:], in_=stock.rearrange("(g p t) -> p g t", g=2, t=SLOTS))
+        nc.sync.dma_start(out=stock_across[:], in_=stock[W:N].partition_broadcast(P))
+        load_sold(1)
+
+        prepare_base()
+        demand(0, 0)
         sort_e(1)
-        first(0, 1)
+        demand(0, 1)
         sign_s(0)
         sort_e(2)
-        weave_s(0, 0, "vector")
-        weave_s(0, 1, "scalar")
-        first(0, 2)
-        scale_q(0, 0, "vector")
-        quant_s(0, 0)
+        demand(0, 2)
+        weave_s(0, BY_COLUMNS, "vector")
+        weave_s(0, BY_ROWS, "scalar")
         sort_e(3)
-        quant_q(0, 0)
-        sign_s(1)
-        quant_s(0, 1)
-        weave_s(1, 0, "vector")
-        weave_s(1, 1, "scalar")
-        first(0, 3)
-        passes(0, 0, 0, "held")
-        scale_q(0, 1, "vector")
-        quant_s(1, 0)
-        sign_s(2)
-        quant_q(0, 1)
-        weave_s(2, 0, "vector")
-        quant_s(1, 1)
-        weave_s(2, 1, "scalar")
-        first(1, 0)
-        passes(0, 0, 1)
-        scale_q(0, 2, "vector")
-        quant_s(2, 0)
-        sign_s(3)
-        quant_q(0, 2)
-        weave_s(3, 0, "vector")
-        quant_s(2, 1)
-        weave_s(3, 1, "scalar")
-        first(1, 1)
-        passes(0, 0, 2)
-        scale_q(0, 3, "vector")
-        quant_s(3, 0)
-        quant_q(0, 3)
-        turn_pre(0, 0)
-        first(1, 2)
-        passes(0, 0, 3)
-        scale_q(1, 0, "vector")
-        quant_s(3, 1)
-        quant_q(1, 0)
-        cap(0, 0, 0)
-        cap(0, 0, 1)
-        cap(0, 0, 2)
-        cap(0, 0, 3)
-        first(1, 3)
-        scale_q(1, 1, "vector")
-        rows_all(0, 1, 0, "held")
-        rows_all(0, 1, 1, "held")
-        turn_y(0, 0, [0,1], "scalar", "quick")
-        turn_y(0, 0, [2,3], "scalar", "quick")
-        quant_q(1, 1)
-        scale_q(1, 2, "vector")
-        rows_cap(0, 1, 0)
-        quant_q(1, 2)
-        rows_add(0, 1, 0)
-        scale_q(1, 3, "vector")
-        weave_y(0, 0, "scalar")
-        rows_all(0, 1, 2, "held")
-        rows_all(0, 1, 3, "held")
-        turn_pre(1, 0)
-        rows_cap(0, 1, 1)
-        quant_q(1, 3)
-        rows_add(0, 1, 1)
-        rows_sort(0, 1, 0, "scalar")
-        rows_sort(0, 1, 1, "scalar")
-        rows_cap(0, 1, 2)
-        quant_y(0, 0)
-        rows_add(0, 1, 2)
-        cols_all(1, 0, 0, "held")
-        rows_all(1, 1, 0, "held")
-        rows_turn(0, 1, 0, "quick")
-        rows_cap(0, 1, 3)
-        cap(1, 0, 0)
-        rows_add(0, 1, 3)
-        rows_sort(0, 1, 2, "scalar")
-        rows_sort(0, 1, 3, "scalar")
-        cols_all(1, 0, 1, "held")
-        rows_all(1, 1, 1, "held")
-        rows_cap(1, 1, 0)
-        rows_quant(0, 1, 0)
-        rows_add(1, 1, 0)
-        rows_turn(0, 1, 1, "quick")
-        cap(1, 0, 1)
-        rows_sort(1, 1, 0, "scalar")
-        cols_all(1, 0, 2, "held")
-        rows_all(1, 1, 2, "held")
-        rows_cap(1, 1, 1)
-        rows_quant(0, 1, 1)
-        store_scales(0)
-        rows_add(1, 1, 1)
-        cap(1, 0, 2)
-        rows_sort(1, 1, 1, "scalar")
-        cols_all(1, 0, 3, "held")
-        rows_turn(1, 1, 0, "quick")
-        rows_all(1, 1, 3, "held")
-        rows_cap(1, 1, 2)
-        cap(1, 0, 3)
-        rows_add(1, 1, 2)
-        rows_sort(1, 1, 2, "scalar")
-        turn_y(1, 0, [0,1], "scalar", "quick")
-        turn_y(1, 0, [2,3], "scalar", "quick")
-        rows_cap(1, 1, 3)
-        rows_quant(1, 1, 0)
-        rows_add(1, 1, 3)
-        rows_sort(1, 1, 3, "vector")
-        weave_y(1, 0, "vector")
-        rows_turn(1, 1, 1, "quick")
-        quant_y(1, 0)
-        rows_quant(1, 1, 1)
-        store_scales(1)
+        weave_q(0, 0, "vector")
+        quantise_s(0, BY_COLUMNS)
+        demand(0, 3)
+        demand(1, 0)
+        last = F_PASSES - 1
+        for f in range(1, F_PASSES):
+            sign_s(f)
+            quantise_q(0, f - 1)
+            weave_s(f, BY_COLUMNS, "vector")
+            column_passes_of_streams(0, f - 1)
+            weave_q(0, f, "vector")
+            quantise_s(f, BY_COLUMNS)
+            quantise_s(f - 1, BY_ROWS)
+            if f == last - 1:
+                turn_sold(0)
+            if f < last:
+                weave_s(f, BY_ROWS, "scalar")
+            demand(1, f)
+        weave_s(last, BY_ROWS, "vector")
+        quantise_q(0, last)
+        column_passes_of_streams(0, last)
+
+        weave_q(1, 1, "scalar")
+        quantise_s(last, BY_ROWS)
+        weave_q(1, 0, "vector")
+        weave_q(1, 2, "scalar")
+        finish_columns(0)
+        row_bank(0, 0, "short")
+        row_bank(0, 1, "short")
+        turn_sold(1)
+        cap_rows(0, 0)
+        quantise_q(1, 0)
+        quantise_q(1, 1)
+        weave_q(1, 3, "vector")
+        row_bank(0, 2, "long")
+        row_bank(0, 3, "long")
+        turn_columns(0, 0, "long")
+        turn_columns(0, 1, "short")
+        quantise_q(1, 2)
+        quantise_q(1, 3)
+        weave_columns(0, "scalar")
+        add_rows(0, 0)
+        cap_rows(0, 1)
+        add_rows(0, 1)
+        round_rows(0)
+
+        row_bank(1, 0, "short")
+        row_bank(1, 1, "short")
+        row_bank(1, 2, "long")
+        row_bank(1, 3, "long")
+        quantise_y(0, BY_COLUMNS)
+        cap_rows(1, 0)
+        add_rows(1, 0)
+        column_bank(1, 0, "long")
+        turn_rows(0, "short")
+        column_bank(1, 1, "long")
+        cap_rows(1, 1)
+        add_rows(1, 1)
+        column_bank(1, 2, "short")
+        column_bank(1, 3, "short")
+        round_rows(1)
+        quantise_y(0, BY_ROWS)
+        turn_rows(1, "long")
+        finish_columns(1)
+        weave_columns(1, "vector")
+        turn_columns(1, 0, "short")
+        quantise_y(1, BY_ROWS)
+        turn_columns(1, 1, "short")
+        quantise_y(1, BY_COLUMNS)
+        store_plane()

@@ -353,13 +353,13 @@ def tile_capped_substitution_demand_h2_kernel(
         load_e(2)
         load_e(3)
         load_s(1)
-        load_s(2)
         load_x(1)
+        load_s(2)
         load_s(3)
         load_sold(0)
         nc.sync.dma_start(out=stock_down[:], in_=stock.rearrange("(g p t) -> p g t", g=2, t=SLOTS))
-        nc.sync.dma_start(out=stock_across[:], in_=stock[W:N].partition_broadcast(P))
         load_sold(1)
+        nc.sync.dma_start(out=stock_across[:], in_=stock[W:N].partition_broadcast(P))
 
         prepare_base()
         demand(0, 0)
@@ -384,11 +384,10 @@ def tile_capped_substitution_demand_h2_kernel(
             weave_q(0, f, "vector")
             quantise_s(f, BY_COLUMNS)
             quantise_s(f - 1, BY_ROWS)
-            if f == last - 1:
-                turn_sold(0)
             if f < last:
                 weave_s(f, BY_ROWS, "scalar")
             demand(1, f)
+        turn_sold(0)
         weave_s(last, BY_ROWS, "vector")
         quantise_q(0, last)
         column_passes_of_streams(0, last)

@@ -23,6 +23,7 @@ W = 512
 K_PASSES = K // W
 F_PASSES = F // W
 BY_COLUMNS, BY_ROWS = 0, 1
+PLAIN_PASSES = 1
 LN2 = math.log(2.0)
 
 
@@ -64,8 +65,7 @@ def tile_capped_substitution_demand_h2_kernel(
         base_padded = kept("base_padded", [P, SLOTS, P], F32)
         log_base = kept("log_base", [P, F_PASSES * SLOTS], F32)
         sign_base = kept("sign_base", [P, F_PASSES * SLOTS], F32)
-        stock_down = kept("stock_down", [P, 2, SLOTS], BF16)
-        warm = kept("warm", [P, 8], F32)
+        stock_down = kept("stock_down", [P, SLOTS], BF16)
         y_plane = kept("y_plane", [P, M], U8)
         stock_across = kept("stock_across", [P, W], BF16)
         s_codes, s_plane, q_codes, q_plane = {}, {}, {}, {}
@@ -86,15 +86,36 @@ def tile_capped_substitution_demand_h2_kernel(
             nc.sync.dma_start(out=e_loaded[f][:], in_=src.bitcast(I32))
 
         def load_s(f):
-            rows = subst.rearrange("(f q t r) n -> f t q r n", f=F_PASSES, t=SLOTS, r=8)
-            for t in range(SLOTS):
-                nc.sync.dma_start(out=s_rows[f][:, t, :], in_=rows[f, t])
+            rows = subst[W * f : W * (f + 1), :]
+            if f < PLAIN_PASSES:
+                nc.sync.dma_start(out=s_rows[f][:], in_=rows.rearrange("(p t) n -> p t n", t=SLOTS))
+            else:
+                runs = rows.rearrange("(q t r) n -> t q r n", t=SLOTS, r=8)
+                for t in range(SLOTS):
+                    nc.sync.dma_start(out=s_rows[f][:, t, :], in_=runs[t])
 
         def load_sold(h):
             src = presold[W * h : W * (h + 1), :].rearrange("(j p) n -> p j n", p=P)
             nc.sync.dma_start(out=sold[h][:], in_=src)
 
         def sort_e(f):
+            if f < PLAIN_PASSES:
+                sort_e_by_columns(f)
+            else:
+                sort_e_by_runs(f)
+
+        def sort_e_by_columns(f):
+            nc.vector.tensor_copy(
+                out=e_plane[f][:].rearrange("p g (t a b) -> p g a t b", t=SLOTS, b=4),
+                in_=e_plane_loaded[:, :, W * f : W * (f + 1)].rearrange("p g (a b t) -> p g a t b", t=SLOTS, b=4),
+            )
+            for g in range(K_PASSES):
+                nc.vector.tensor_copy(
+                    out=e_codes[f][:, g, :].rearrange("p (t a b w) -> p a t b w", t=SLOTS, b=2, w=2),
+                    in_=e_loaded[f][:, g, :].bitcast(U8).rearrange("p (a b t w) -> p a t b w", t=SLOTS, b=2, w=2),
+                )
+
+        def sort_e_by_runs(f):
             nc.vector.tensor_copy(
                 out=e_codes[f][:].bitcast(I32).rearrange("p g (t q w) -> p g t q w", t=SLOTS, w=4),
                 in_=e_loaded[f][:].rearrange("p g (q t w) -> p g t q w", t=SLOTS, w=4),
@@ -109,6 +130,10 @@ def tile_capped_substitution_demand_h2_kernel(
             nc.vector.tensor_copy(
                 out=base_padded[0:F_PASSES, :, :].rearrange("f t (q r) -> f t q r", r=8),
                 in_=base_rows[:].rearrange("f (q t r) -> f t q r", t=SLOTS, r=8),
+            )
+            nc.vector.tensor_copy(
+                out=base_padded[0:PLAIN_PASSES, :, :],
+                in_=base_rows[0:PLAIN_PASSES, :].rearrange("f (p t) -> f t p", t=SLOTS),
             )
             acc = bank("short")
             for t in range(SLOTS):
@@ -139,14 +164,14 @@ def tile_capped_substitution_demand_h2_kernel(
             nc.vector.tensor_scalar(out=d, in0=ratio, scalar1=-1.0, scalar2=None, op0=ALU.add)
             nc.vector.tensor_scalar(out=p0, in0=ratio, scalar1=0.2, scalar2=-0.2 - 0.25, op0=ALU.mult, op1=ALU.add)
             nc.vector.tensor_tensor(out=p1, in0=p0, in1=d, op=ALU.mult)
-            sort_e(0)
+            sort_e(1)
             nc.vector.scalar_tensor_tensor(out=p2, in0=p1, scalar=1.0 / 3.0, in1=d, op0=ALU.add, op1=ALU.mult)
             nc.vector.scalar_tensor_tensor(out=p3, in0=p2, scalar=-0.5, in1=d, op0=ALU.add, op1=ALU.mult)
             nc.vector.scalar_tensor_tensor(out=p0, in0=p3, scalar=1.0, in1=d, op0=ALU.add, op1=ALU.mult)
             nc.vector.tensor_tensor(out=log_base[:], in0=p0, in1=guess, op=ALU.add)
 
         def demand(h, f):
-            q_slots[h, f] = reused("q_slots", [P, SLOTS, W], BF16, 4)
+            q_slots[h, f] = reused("q_slots", [P, SLOTS, W], BF16, 5)
             for t in range(SLOTS):
                 acc = bank("short")
                 for g in range(K_PASSES):
@@ -251,7 +276,7 @@ def tile_capped_substitution_demand_h2_kernel(
                 for j in range(4):
                     words = sold[h][:, j, :].bitcast(F32)
                     nc.tensor.transpose(acc[:, P * j : P * (j + 1)], words[:, u : W // 2 : 2], ident[:])
-                sold_turned[h, u] = reused("sold_turned", [P, W], F32, 4)
+                sold_turned[h, u] = reused("sold_turned", [P, W], F32, 2)
                 nc.scalar.copy(out=sold_turned[h, u][:], in_=acc[:])
 
         def finish_columns(h):
@@ -260,7 +285,7 @@ def tile_capped_substitution_demand_h2_kernel(
                 nc.vector.scalar_tensor_tensor(
                     out=y_columns[h][:, t, :],
                     in0=u_bank[h, BY_COLUMNS, t][:],
-                    scalar=stock_down[:, BY_COLUMNS, t : t + 1],
+                    scalar=stock_down[:, t : t + 1],
                     in1=sold_turned[h, t // 2][:].bitcast(BF16)[:, t % 2 :: 2],
                     op0=ALU.min,
                     op1=ALU.add,
@@ -280,7 +305,7 @@ def tile_capped_substitution_demand_h2_kernel(
             store_rows(h, BY_COLUMNS, pair)
 
         def weave_columns(h, engine):
-            y_woven[h, BY_COLUMNS] = reused("y_woven", [P, SLOTS * W], BF16, 2)
+            y_woven[h, BY_COLUMNS] = reused("y_woven", [P, SLOTS * W], BF16, 3)
             weave(engine, y_woven[h, BY_COLUMNS][:], y_columns[h][:])
 
         def row_bank(h, j, bank_set):
@@ -321,7 +346,7 @@ def tile_capped_substitution_demand_h2_kernel(
                 )
 
         def turn_rows(h, bank_set):
-            y_woven[h, BY_ROWS] = reused("y_woven", [P, SLOTS * W], BF16, 2)
+            y_woven[h, BY_ROWS] = reused("y_woven", [P, SLOTS * W], BF16, 3)
             for pair in range(2):
                 acc = bank(bank_set)
                 for i in range(2):
@@ -338,17 +363,15 @@ def tile_capped_substitution_demand_h2_kernel(
         nc.gpsimd.memset(x_plane[:].bitcast(I32), 0)
         nc.vector.memset(e_plane_loaded[:].bitcast(I32), 0)
         nc.vector.memset(ident[:], 0.0)
-        nc.vector.memset(warm[:], 0.0)
-        nc.scalar.activation(out=warm[:, 0:1], in_=warm[:, 1:2], func=ACT.Exp)
         make_identity(nc, ident[:], nomemset=True)
         nc.vector.memset(base_padded[:], 0.0)
 
         nc.sync.dma_start(out=base_rows[:], in_=base.rearrange("(f k) -> f k", f=F_PASSES))
         load_scale_rows(x_plane, x_scales)
         load_scale_rows(e_plane_loaded, e_scales)
-        load_e(0)
-        load_x(0)
         load_e(1)
+        load_x(0)
+        load_e(0)
         load_s(0)
         load_e(2)
         load_e(3)
@@ -357,14 +380,14 @@ def tile_capped_substitution_demand_h2_kernel(
         load_s(2)
         load_s(3)
         load_sold(0)
-        nc.sync.dma_start(out=stock_down[:], in_=stock.rearrange("(g p t) -> p g t", g=2, t=SLOTS))
+        nc.sync.dma_start(out=stock_down[:], in_=stock[0:W].rearrange("(p t) -> p t", t=SLOTS))
         load_sold(1)
         nc.sync.dma_start(out=stock_across[:], in_=stock[W:N].partition_broadcast(P))
 
         prepare_base()
-        demand(0, 0)
-        sort_e(1)
         demand(0, 1)
+        sort_e(0)
+        demand(0, 0)
         sign_s(0)
         sort_e(2)
         demand(0, 2)
@@ -388,8 +411,8 @@ def tile_capped_substitution_demand_h2_kernel(
                 weave_s(f, BY_ROWS, "scalar")
             demand(1, f)
         turn_sold(0)
-        weave_s(last, BY_ROWS, "vector")
         quantise_q(0, last)
+        weave_s(last, BY_ROWS, "vector")
         column_passes_of_streams(0, last)
 
         weave_q(1, 1, "scalar")
@@ -420,8 +443,8 @@ def tile_capped_substitution_demand_h2_kernel(
         row_bank(1, 1, "short")
         row_bank(1, 2, "long")
         row_bank(1, 3, "long")
-        quantise_y(0, BY_COLUMNS)
         cap_rows(1, 0)
+        quantise_y(0, BY_COLUMNS)
         add_rows(1, 0)
         column_bank(1, 0, "long")
         turn_rows(0, "short")
@@ -431,9 +454,9 @@ def tile_capped_substitution_demand_h2_kernel(
         column_bank(1, 2, "short")
         column_bank(1, 3, "short")
         round_rows(1)
-        quantise_y(0, BY_ROWS)
         turn_rows(1, "long")
         finish_columns(1)
+        quantise_y(0, BY_ROWS)
         weave_columns(1, "vector")
         turn_columns(1, 0, "short")
         quantise_y(1, BY_ROWS)

import math
from contextlib import ExitStack

import concourse.mybir as mybir
from concourse.masks import make_identity

M, K, F, N = 1024, 1024, 2048, 1024
FLOPS = 2 * M * K * F + 2 * M * F * N

F32 = mybir.dt.float32
BF16 = mybir.dt.bfloat16
I32 = mybir.dt.int32
U32 = mybir.dt.uint32
U8 = mybir.dt.uint8
FP8X4 = mybir.dt.float8_e4m3fn_x4
FP4X4 = mybir.dt.float4_e2m1fn_x4
ALU = mybir.AluOpType
ACT = mybir.ActivationFunctionType

P = 128
SLOTS = 4
W = 512
K_PASSES = K // W
F_PASSES = F // W
BY_COLUMNS, BY_ROWS = 0, 1
PLAIN_PASSES = 1
LN2 = math.log(2.0)


def tile_capped_substitution_demand_h2_kernel(
    tc, x_words, x_scales, e_words, e_scales, base, subst, stock, presold, out_0, out_1, out_2
):
    nc = tc.nc
    with ExitStack() as ctx:
        keep = ctx.enter_context(tc.tile_pool(name="keep", bufs=1))
        ring = ctx.enter_context(tc.tile_pool(name="ring", bufs=2))
        psum = ctx.enter_context(tc.psum_pool(name="psum", bufs=4))
        ctx.enter_context(tc.manual_schedule())

        def kept(name, shape, dtype):
            return keep.tile(shape, dtype, name=name, align_bytes=64)

        def reused(tag, shape, dtype, bufs):
            return ring.tile(shape, dtype, name=tag, tag=tag, bufs=bufs, align_bytes=64)

        def bank(bank_set):
            return psum.tile([P, W], F32, name=bank_set, tag=bank_set)

        def move(engine, dst, src):
            if engine == "scalar":
                nc.scalar.copy(out=dst, in_=src)
            else:
                nc.vector.tensor_copy(out=dst, in_=src)

        x_codes = [kept("x_codes%d" % h, [P, K_PASSES, W], U32) for h in range(2)]
        x_plane = kept("x_plane", [P, K_PASSES, M], U8)
        e_loaded = [kept("e_loaded%d" % f, [P, K_PASSES, W // 2], I32) for f in range(F_PASSES)]
        e_plane_loaded = kept("e_plane_loaded", [P, K_PASSES, F], U8)
        e_codes = [kept("e_codes%d" % f, [P, K_PASSES, 2 * W], U8) for f in range(F_PASSES)]
        e_plane = [kept("e_plane%d" % f, [P, K_PASSES, W], U8) for f in range(F_PASSES)]
        s_rows = [kept("s_rows%d" % f, [P, SLOTS, N], BF16) for f in range(F_PASSES)]
        sold = [kept("sold%d" % h, [P, 4, N], BF16) for h in range(2)]
        ident = kept("ident", [P, P], F32)
        base_rows = kept("base_rows", [F_PASSES, W], BF16)
        base_padded = kept("base_padded", [P, SLOTS, P], F32)
        log_base = kept("log_base", [P, F_PASSES * SLOTS], F32)
        sign_base = kept("sign_base", [P, F_PASSES * SLOTS], F32)
        stock_down = kept("stock_down", [P, SLOTS], BF16)
        y_plane = kept("y_plane", [P, M], U8)
        stock_across = kept("stock_across", [P, W], BF16)
        s_codes, s_plane, q_codes, q_plane = {}, {}, {}, {}
        q_slots, q_woven, s_woven, sold_turned, u_bank, y_columns, y_woven = {}, {}, {}, {}, {}, {}, {}
        capped, y_rows, y_pairs = {}, {}, {}

        def load_scale_rows(plane, rows):
            for quad in range(4):
                src = rows[:, 4 * quad : 4 * quad + 4, :].rearrange("g r n -> r g n")
                nc.sync.dma_start(out=plane[32 * quad : 32 * quad + 4, :, :].bitcast(I32), in_=src.bitcast(I32))

        def load_x(h):
            src = x_words.rearrange("g p m t -> p g (m t)")[:, :, SLOTS * W * h : SLOTS * W * (h + 1)]
            nc.sync.dma_start(out=x_codes[h][:].bitcast(I32), in_=src.bitcast(I32))

        def load_e(f):
            src = e_words.rearrange("g p b -> p g b")[:, :, 2 * W * f : 2 * W * (f + 1)]
            nc.sync.dma_start(out=e_loaded[f][:], in_=src.bitcast(I32))

        def load_s(f):
            rows = subst[W * f : W * (f + 1), :]
            if f < PLAIN_PASSES:
                nc.sync.dma_start(out=s_rows[f][:], in_=rows.rearrange("(p t) n -> p t n", t=SLOTS))
            else:
                runs = rows.rearrange("(q t r) n -> t q r n", t=SLOTS, r=8)
                for t in range(SLOTS):
                    nc.sync.dma_start(out=s_rows[f][:, t, :], in_=runs[t])

        def load_sold(h):
            src = presold[W * h : W * (h + 1), :].rearrange("(j p) n -> p j n", p=P)
            nc.sync.dma_start(out=sold[h][:], in_=src)

        def sort_e(f):
            if f < PLAIN_PASSES:
                sort_e_by_columns(f)
            else:
                sort_e_by_runs(f)

        def sort_e_by_columns(f):
            nc.vector.tensor_copy(
                out=e_plane[f][:].rearrange("p g (t a b) -> p g a t b", t=SLOTS, b=4),
                in_=e_plane_loaded[:, :, W * f : W * (f + 1)].rearrange("p g (a b t) -> p g a t b", t=SLOTS, b=4),
            )
            for g in range(K_PASSES):
                nc.vector.tensor_copy(
                    out=e_codes[f][:, g, :].rearrange("p (t a b w) -> p a t b w", t=SLOTS, b=2, w=2),
                    in_=e_loaded[f][:, g, :].bitcast(U8).rearrange("p (a b t w) -> p a t b w", t=SLOTS, b=2, w=2),
                )

        def sort_e_by_runs(f):
            nc.vector.tensor_copy(
                out=e_codes[f][:].bitcast(I32).rearrange("p g (t q w) -> p g t q w", t=SLOTS, w=4),
                in_=e_loaded[f][:].rearrange("p g (q t w) -> p g t q w", t=SLOTS, w=4),
            )
            loaded = e_plane_loaded[:, :, W * f : W * (f + 1)].bitcast(I32)
            nc.vector.tensor_copy(
                out=e_plane[f][:].bitcast(I32).rearrange("p g (t q w) -> p g t q w", t=SLOTS, w=2),
                in_=loaded.rearrange("p g (q t w) -> p g t q w", t=SLOTS, w=2),
            )

        def prepare_base():
            nc.vector.tensor_copy(
                out=base_padded[0:F_PASSES, :, :].rearrange("f t (q r) -> f t q r", r=8),
                in_=base_rows[:].rearrange("f (q t r) -> f t q r", t=SLOTS, r=8),
            )
            nc.vector.tensor_copy(
                out=base_padded[0:PLAIN_PASSES, :, :],
                in_=base_rows[0:PLAIN_PASSES, :].rearrange("f (p t) -> f t p", t=SLOTS),
            )
            acc = bank("short")
            for t in range(SLOTS):
                nc.tensor.transpose(acc[:, P * t : P * (t + 1)], base_padded[:, t, :], ident[:])
            values = acc[:].rearrange("p (t f) -> p f t", t=SLOTS)[:, 0:F_PASSES, :]
            small = [kept("small%d" % i, [P, F_PASSES * SLOTS], F32) for i in range(10)]
            negative, size, guess, inverse, ratio, d, p0, p1, p2, p3 = [tile[:] for tile in small]
            nc.scalar.activation(out=size.rearrange("p (f t) -> p f t", t=SLOTS), in_=values, func=ACT.Abs)
            nc.vector.tensor_scalar(
                out=negative.rearrange("p (f t) -> p f t", t=SLOTS),
                in0=values,
                scalar1=0.0,
                scalar2=-2.0,
                op0=ALU.is_lt,
                op1=ALU.mult,
            )
            nc.vector.tensor_scalar(
                out=guess,
                in0=size.bitcast(I32),
                scalar1=LN2 / 2**23,
                scalar2=0.03 - 127 * LN2,
                op0=ALU.mult,
                op1=ALU.add,
            )
            nc.scalar.activation(out=inverse, in_=guess, func=ACT.Exp, scale=-1.0)
            nc.vector.tensor_scalar(out=sign_base[:], in0=negative, scalar1=1.0, scalar2=None, op0=ALU.add)
            nc.vector.tensor_tensor(out=ratio, in0=size, in1=inverse, op=ALU.mult)
            nc.vector.tensor_scalar(out=d, in0=ratio, scalar1=-1.0, scalar2=None, op0=ALU.add)
            nc.vector.tensor_scalar(out=p0, in0=ratio, scalar1=0.2, scalar2=-0.2 - 0.25, op0=ALU.mult, op1=ALU.add)
            nc.vector.tensor_tensor(out=p1, in0=p0, in1=d, op=ALU.mult)
            sort_e(1)
            nc.vector.scalar_tensor_tensor(out=p2, in0=p1, scalar=1.0 / 3.0, in1=d, op0=ALU.add, op1=ALU.mult)
            nc.vector.scalar_tensor_tensor(out=p3, in0=p2, scalar=-0.5, in1=d, op0=ALU.add, op1=ALU.mult)
            nc.vector.scalar_tensor_tensor(out=p0, in0=p3, scalar=1.0, in1=d, op0=ALU.add, op1=ALU.mult)
            nc.vector.tensor_tensor(out=log_base[:], in0=p0, in1=guess, op=ALU.add)

        def demand(h, f):
            q_slots[h, f] = reused("q_slots", [P, SLOTS, W], BF16, 5)
            for t in range(SLOTS):
                acc = bank("short")
                for g in range(K_PASSES):
                    nc.tensor.matmul_mx(
                        out=acc[:],
                        lhsT=e_codes[f][:, g, 2 * P * t : 2 * P * (t + 1)].bitcast(FP4X4),
                        lhsT_scale=e_plane[f][:, g, P * t : P * (t + 1)],
                        rhs=x_codes[h][:, g, :].bitcast(FP8X4),
                        rhs_scale=x_plane[:, g, W * h : W * (h + 1)],
                        start=(g == 0),
                        stop=(g == K_PASSES - 1),
                    )
                column = SLOTS * f + t
                nc.scalar.activation(
                    out=q_slots[h, f][:, t, :], in_=acc[:], func=ACT.Exp, bias=log_base[:, column : column + 1]
                )

        def weave(engine, dst, src):
            move(
                engine,
                dst.rearrange("p (c i t) -> p c t i", i=4, t=SLOTS),
                src.rearrange("p t (c i) -> p c t i", i=4),
            )

        def weave_q(h, f, engine):
            q_woven[h, f] = reused("q_woven", [P, SLOTS * W], BF16, 3)
            weave(engine, q_woven[h, f][:], q_slots[h, f][:])

        def quantise_q(h, f):
            q_codes[h, f] = kept("q_codes%d%d" % (h, f), [P, W], U32)
            q_plane[h, f] = kept("q_plane%d%d" % (h, f), [P, W], U8)
            nc.vector.quantize_mx(out=q_codes[h, f][:].bitcast(FP8X4), scales=q_plane[h, f][:], in_=q_woven[h, f][:])

        def sign_s(f):
            for t in range(SLOTS):
                row = s_rows[f][:, t, :]
                column = SLOTS * f + t
                nc.vector.tensor_scalar(
                    out=row, in0=row, scalar1=sign_base[:, column : column + 1], scalar2=None, op0=ALU.mult
                )

        def weave_s(f, g, engine):
            s_woven[f, g] = reused("s_woven", [P, SLOTS * W], BF16, 3)
            src = s_rows[f][:, :, W * g : W * (g + 1)]
            if g == BY_ROWS:
                weave(engine, s_woven[f, g][:], src)
            else:
                move(
                    engine,
                    s_woven[f, g][:].rearrange("p (u a b t) -> p u a t b", u=SLOTS, b=2, t=SLOTS),
                    src.rearrange("p t (a b u) -> p u a t b", b=2, u=SLOTS),
                )

        def quantise_s(f, g):
            s_codes[f, g] = kept("s_codes%d%d" % (f, g), [P, W], U32)
            s_plane[f, g] = kept("s_plane%d%d" % (f, g), [P, W], U8)
            nc.vector.quantize_mx(out=s_codes[f, g][:].bitcast(FP8X4), scales=s_plane[f, g][:], in_=s_woven[f, g][:])

        def store_rows(h, g, pair):
            m0 = W * h + 2 * P * pair
            dst = out_0[m0 : m0 + 2 * P, W * g : W * (g + 1)].rearrange("(j p) n -> p j n", p=P)
            nc.sync.dma_start(out=dst, in_=y_rows[h, g, pair][:])

        def quantise_y(h, g):
            y_codes = reused("y_codes", [P, W], U32, 3)
            nc.vector.quantize_mx(
                out=y_codes[:].bitcast(FP8X4), scales=y_plane[4 * g : P, W * h : W * (h + 1)], in_=y_woven[h, g][:]
            )
            dst = out_1[g].rearrange("p m t -> p (m t)")[:, SLOTS * W * h : SLOTS * W * (h + 1)]
            nc.sync.dma_start(out=dst.bitcast(I32), in_=y_codes[:].bitcast(I32))

        def store_plane():
            for quad in range(4):
                dst = out_2[:, 4 * quad : 4 * quad + 4, :]
                nc.sync.dma_start(out=dst.bitcast(I32), in_=y_plane[32 * quad : 32 * quad + 8, :].bitcast(I32))

        def column_pass(h, t, f):
            nc.tensor.matmul_mx(
                out=u_bank[h, BY_COLUMNS, t][:],
                lhsT=s_codes[f, BY_COLUMNS][:, P * t : P * (t + 1)].bitcast(FP8X4),
                lhsT_scale=s_plane[f, BY_COLUMNS][:, P * t : P * (t + 1)],
                rhs=q_codes[h, f][:].bitcast(FP8X4),
                rhs_scale=q_plane[h, f][:],
                start=(f == 0),
                stop=(f == F_PASSES - 1),
            )

        def column_passes_of_streams(h, f):
            for t in range(SLOTS):
                if f == 0:
                    u_bank[h, BY_COLUMNS, t] = bank("long")
                column_pass(h, t, f)

        def column_bank(h, t, bank_set):
            u_bank[h, BY_COLUMNS, t] = bank(bank_set)
            for f in range(F_PASSES):
                column_pass(h, t, f)

        def turn_sold(h):
            for u in range(2):
                acc = bank("short")
                for j in range(4):
                    words = sold[h][:, j, :].bitcast(F32)
                    nc.tensor.transpose(acc[:, P * j : P * (j + 1)], words[:, u : W // 2 : 2], ident[:])
                sold_turned[h, u] = reused("sold_turned", [P, W], F32, 2)
                nc.scalar.copy(out=sold_turned[h, u][:], in_=acc[:])

        def finish_columns(h):
            y_columns[h] = reused("y_columns", [P, SLOTS, W], F32, 2)
            for t in range(SLOTS):
                nc.vector.scalar_tensor_tensor(
                    out=y_columns[h][:, t, :],
                    in0=u_bank[h, BY_COLUMNS, t][:],
                    scalar=stock_down[:, t : t + 1],
                    in1=sold_turned[h, t // 2][:].bitcast(BF16)[:, t % 2 :: 2],
                    op0=ALU.min,
                    op1=ALU.add,
                )

        def turn_columns(h, pair, bank_set):
            y_rows[h, BY_COLUMNS, pair] = reused("y_rows", [P, 2, W], F32, 4)
            for i in range(2):
                j = 2 * pair + i
                acc = bank(bank_set)
                for t in range(SLOTS):
                    nc.tensor.transpose(acc[:, P * t : P * (t + 1)], y_columns[h][:, t, P * j : P * (j + 1)], ident[:])
                nc.scalar.copy(
                    out=y_rows[h, BY_COLUMNS, pair][:, i, :].rearrange("p (n t) -> p n t", t=SLOTS),
                    in_=acc[:].rearrange("p (t n) -> p n t", t=SLOTS),
                )
            store_rows(h, BY_COLUMNS, pair)

        def weave_columns(h, engine):
            y_woven[h, BY_COLUMNS] = reused("y_woven", [P, SLOTS * W], BF16, 3)
            weave(engine, y_woven[h, BY_COLUMNS][:], y_columns[h][:])

        def row_bank(h, j, bank_set):
            u_bank[h, BY_ROWS, j] = bank(bank_set)
            for f in range(F_PASSES):
                nc.tensor.matmul_mx(
                    out=u_bank[h, BY_ROWS, j][:],
                    lhsT=q_codes[h, f][:, P * j : P * (j + 1)].bitcast(FP8X4),
                    lhsT_scale=q_plane[h, f][:, P * j : P * (j + 1)],
                    rhs=s_codes[f, BY_ROWS][:].bitcast(FP8X4),
                    rhs_scale=s_plane[f, BY_ROWS][:],
                    start=(f == 0),
                    stop=(f == F_PASSES - 1),
                )

        def cap_rows(h, pair):
            for j in (2 * pair, 2 * pair + 1):
                capped[h, j] = reused("capped", [P, W], F32, 2)
                nc.vector.tensor_tensor(
                    out=capped[h, j][:], in0=u_bank[h, BY_ROWS, j][:], in1=stock_across[:], op=ALU.min
                )

        def add_rows(h, pair):
            y_rows[h, BY_ROWS, pair] = reused("y_rows", [P, 2, W], F32, 4)
            for i in range(2):
                j = 2 * pair + i
                nc.vector.tensor_tensor(
                    out=y_rows[h, BY_ROWS, pair][:, i, :], in0=capped[h, j][:], in1=sold[h][:, j, W:N], op=ALU.add
                )
            store_rows(h, BY_ROWS, pair)

        def round_rows(h):
            for j in range(4):
                y_pairs[h, j] = reused("y_pairs", [P, W], BF16, 4)
                nc.scalar.copy(
                    out=y_pairs[h, j][:].rearrange("p (u n e) -> p u n e", u=2, e=2),
                    in_=y_rows[h, BY_ROWS, j // 2][:, j % 2, :].rearrange("p (n u e) -> p u n e", u=2, e=2),
                )

        def turn_rows(h, bank_set):
            y_woven[h, BY_ROWS] = reused("y_woven", [P, SLOTS * W], BF16, 3)
            for pair in range(2):
                acc = bank(bank_set)
                for i in range(2):
                    words = y_pairs[h, 2 * pair + i][:].bitcast(F32)
                    for u in range(2):
                        c0 = P * (2 * i + u)
                        nc.tensor.transpose(acc[:, c0 : c0 + P], words[:, P * u : P * (u + 1)], ident[:])
                dst = y_woven[h, BY_ROWS][:, 2 * W * pair : 2 * W * (pair + 1)].bitcast(F32)
                nc.scalar.copy(
                    out=dst.rearrange("p (i m u) -> p i m u", i=2, u=2),
                    in_=acc[:].rearrange("p (i u m) -> p i m u", i=2, u=2),
                )

        nc.gpsimd.memset(x_plane[:].bitcast(I32), 0)
        nc.vector.memset(e_plane_loaded[:].bitcast(I32), 0)
        nc.vector.memset(ident[:], 0.0)
        make_identity(nc, ident[:], nomemset=True)
        nc.vector.memset(base_padded[:], 0.0)

        nc.sync.dma_start(out=base_rows[:], in_=base.rearrange("(f k) -> f k", f=F_PASSES))
        load_scale_rows(x_plane, x_scales)
        load_scale_rows(e_plane_loaded, e_scales)
        load_e(1)
        load_x(0)
        load_e(0)
        load_s(0)
        load_e(2)
        load_e(3)
        load_s(1)
        load_x(1)
        load_s(2)
        load_s(3)
        load_sold(0)
        nc.sync.dma_start(out=stock_down[:], in_=stock[0:W].rearrange("(p t) -> p t", t=SLOTS))
        load_sold(1)
        nc.sync.dma_start(out=stock_across[:], in_=stock[W:N].partition_broadcast(P))

        prepare_base()
        demand(0, 1)
        sort_e(0)
        demand(0, 0)
        sign_s(0)
        sort_e(2)
        demand(0, 2)
        weave_s(0, BY_COLUMNS, "vector")
        weave_s(0, BY_ROWS, "scalar")
        sort_e(3)
        weave_q(0, 0, "vector")
        quantise_s(0, BY_COLUMNS)
        demand(0, 3)
        demand(1, 0)
        last = F_PASSES - 1
        for f in range(1, F_PASSES):
            sign_s(f)
            quantise_q(0, f - 1)
            weave_s(f, BY_COLUMNS, "vector")
            column_passes_of_streams(0, f - 1)
            weave_q(0, f, "vector")
            quantise_s(f, BY_COLUMNS)
            quantise_s(f - 1, BY_ROWS)
            if f < last:
                weave_s(f, BY_ROWS, "scalar")
            demand(1, f)
        turn_sold(0)
        quantise_q(0, last)
        weave_s(last, BY_ROWS, "vector")
        column_passes_of_streams(0, last)

        weave_q(1, 1, "scalar")
        quantise_s(last, BY_ROWS)
        weave_q(1, 0, "vector")
        weave_q(1, 2, "scalar")
        finish_columns(0)
        row_bank(0, 0, "short")
        row_bank(0, 1, "short")
        turn_sold(1)
        cap_rows(0, 0)
        quantise_q(1, 0)
        quantise_q(1, 1)
        weave_q(1, 3, "vector")
        row_bank(0, 2, "long")
        row_bank(0, 3, "long")
        turn_columns(0, 0, "long")
        turn_columns(0, 1, "short")
        quantise_q(1, 2)
        quantise_q(1, 3)
        weave_columns(0, "scalar")
        add_rows(0, 0)
        cap_rows(0, 1)
        add_rows(0, 1)
        round_rows(0)

        row_bank(1, 0, "short")
        row_bank(1, 1, "short")
        row_bank(1, 2, "long")
        row_bank(1, 3, "long")
        cap_rows(1, 0)
        quantise_y(0, BY_COLUMNS)
        add_rows(1, 0)
        column_bank(1, 0, "long")
        turn_rows(0, "short")
        column_bank(1, 1, "long")
        cap_rows(1, 1)
        add_rows(1, 1)
        column_bank(1, 2, "short")
        column_bank(1, 3, "short")
        round_rows(1)
        turn_rows(1, "long")
        finish_columns(1)
        quantise_y(0, BY_ROWS)
        weave_columns(1, "vector")
        turn_columns(1, 0, "short")
        quantise_y(1, BY_ROWS)
        turn_columns(1, 1, "short")
        quantise_y(1, BY_COLUMNS)
        store_plane()
